import numpy as np, ml_dtypes
CORES = [2,6,10,14,18,22,26,30]
N = 8
import mx_ref
BF = ml_dtypes.bfloat16
def entries(a):
    return np.ascontiguousarray(a.T).reshape(-1)
def table(e):
    return np.ascontiguousarray(np.reshape(e, (-1, 16)).T).astype(np.int32)
def gcols(t, e):
    v = np.concatenate([t.reshape(8, 16, -1, 4), np.zeros((8, 16, 1, 4), BF)], axis=2)
    return np.ascontiguousarray(np.stack([v[g][:, e[g]] for g in range(8)])).reshape(128, -1)
def tile(rs):
    return np.stack(rs, axis=2).reshape(128, -1).astype(BF)
def pick(q, e):
    c = np.concatenate([q[0].reshape(128, -1, 4), np.zeros((128, 1, 4), np.uint8)], axis=1); s = np.concatenate([q[1], np.ones((16, 1), np.uint8)], axis=1)
    return (np.ascontiguousarray(c[:, e].reshape(128, -1)), np.ascontiguousarray(s[:, e]))
def join(*qs):
    return (np.concatenate([q[0] for q in qs], axis=1), np.concatenate([q[1] for q in qs], axis=1))
def put(q, e, v):
    c, s = q[0].reshape(128, -1, 4).copy(), q[1].copy(); c[:, e] = v[0].reshape(128, -1, 4); s[:, e] = v[1]
    return (c.reshape(128, -1), s)
def pk(c, s):
    return (np.ascontiguousarray(c), mx_ref.live(s))
def emit(q):
    return q[0], q[1]
def packed(v, rng):
    q = [mx_ref.quantize(np.ascontiguousarray(v[r])) for r in range(N)]
    return np.stack([a for a, b in q]), np.stack([mx_ref.plane(b, rng) for a, b in q])
def values_of_codes():
    e, c = np.zeros((128, 128, 4), np.float32), np.zeros((128, 2, 4), np.uint8)
    e[np.arange(128), np.arange(128), 0] = 1
    c[:127, :, 0] = np.arange(256).reshape(2, 128).T[:127]
    return mx_ref.matmul(mx_ref.quantize(e.reshape(128, 512).astype(BF)), (c.reshape(128, 8), np.full((16, 2), 127, np.uint8))).T.reshape(-1).astype(np.float64)
CODE_VALUE, SCALE_VALUE = values_of_codes(), 2.0 ** (np.arange(256) - 127.0)
def decode(q):
    return (CODE_VALUE[q[0]].reshape(16, 8, -1, 4) * SCALE_VALUE[q[1]][:, None, :, None] + 0.0).reshape(128, -1).astype(np.float32)
def f(rng, *shape):
    return mx_ref.flush((rng.standard_normal(shape, dtype=np.float32) * np.exp2(rng.integers(-2, 3, shape[:-1] + (1,)))).astype(BF))
def wide(rng, *shape, cols=0):
    v = rng.standard_normal(shape, dtype=np.float32) * np.exp2(rng.integers(-12, 13, shape)).astype(np.float32)
    if cols: v *= np.repeat(np.exp2(rng.integers(-cols, cols + 1, shape[:-2] + (1, shape[-1] // 4))) * (rng.random(shape[:-2] + (1, shape[-1] // 4)) > 0.0625), 4, axis=-1).astype(np.float32)
    return mx_ref.flush(v.astype(BF))
C, R = 256, 2
M = N * C
def numbers_of(rng):
    return {"x": np.array(f(rng, N, 128, 4 * C)), "u": np.array(f(rng, N, 128, 512)), "v": np.array(f(rng, N, 128, 512))}
def weights(rng, w):
    c, p = packed(w, rng)
    return {"wc": c, "ws": p}
def still(rng):
    w = np.zeros((N, 128, 4, 128, 4), np.float32)
    i = np.arange(128)
    for b in range(4): w[:, i, b, i, b] = 32
    return weights(rng, w.reshape(N, 128, 2048).astype(BF))
def anywhere(rng):
    return rng.integers(0, M, (4, M))
def stored(e):
    return np.stack([table(e[:, C * r:C * r + C].reshape(-1)) for r in range(N)])
def signs(rng):
    return rng.permutation(N) % 2 * 2.0 - 1.0
def setup_inputs(rng):
    return {**numbers_of(rng), **weights(rng, f(rng, N, 128, 2048)), "sc": stored(anywhere(rng))}
def setup_inputs_ties(rng):
    d = numbers_of(rng)
    x = d["x"].reshape(N, 128, C, 4)
    a = x[0, :8, :3].copy()
    a[:, 2] = 0
    for r in range(N): x[r, :8] = a[:, rng.permutation(C) % 3]
    u = d["u"].reshape(N, 128, 128, 4)
    u[:, :8, 0] = u[0, :8, 0].copy()
    u[:, 8:, 0] = 0
    w = np.array(f(rng, 128, 2048)).reshape(128, 4, 128, 4)
    w[8:, :, :8] = 0
    return {"x": x.reshape(N, 128, 4 * C), "u": u.reshape(N, 128, 512), "v": d["v"], **weights(rng, np.stack([w.reshape(128, 2048)] * N)), "sc": stored(anywhere(rng))}
def setup_inputs_near(rng):
    d = numbers_of(rng)
    g = signs(rng)
    low = np.repeat(g < 0, C)
    o = np.concatenate([rng.permutation(np.flatnonzero(low)), rng.permutation(np.flatnonzero(~low))])
    place = np.argsort(o)
    s = place % (M // 2)
    x = np.abs(d["x"].astype(np.float32)).reshape(N, 128, C, 4)
    v = (((s[:, None] >> np.arange(12)) & 1) * np.exp2(np.arange(12) - 23.0)).reshape(N, C, 12)
    x[:, :8] = 0
    x[:, 0, :, 0] = 1
    for i in range(3): x[:, 8 + i] = v[:, :, 4 * i:4 * i + 4]
    x[:, 11:16] = rng.integers(4, 8, (N, 5, C, 4)) * 2.0 ** -20
    u = d["u"].reshape(N, 128, 128, 4)
    u[:, :, 0] = 0
    u[:, 0, 0, 0] = g.astype(np.float32).astype(BF)
    u[:, 8:11, 0] = 1
    c = rng.permutation(M)
    after = np.zeros(M, int)
    after[c] = np.roll(c, -1)
    e = np.stack([o[np.maximum(place[after] - i, 0)] for i in range(4)])
    e = np.take_along_axis(e, np.argsort(rng.random((4, M)), axis=0), axis=0)
    k = np.flatnonzero(place[after] >= M // 2 + 4)[::2]
    a = place[after[k]]
    e[:, k] = o[np.stack([a - M // 2 - 4, a - 1, a, a - 2])]
    return {"x": x.reshape(N, 128, 4 * C).astype(BF), "u": u.reshape(N, 128, 512), "v": d["v"], **still(rng), "sc": stored(e)}
def setup_inputs_huge(rng):
    d = numbers_of(rng)
    g = signs(rng)
    x = 2.0 ** 30 * (0.6 + 0.4 * rng.random((N, 128, 4 * C)))
    u = d["u"].reshape(N, 128, 128, 4)
    a = 2.0 ** 30 * (1 - 0.25 * rng.random((N, 128, 4))) * g[:, None, None]
    u[:, :, 0] = a.astype(np.float32).astype(BF)
    minus, plus = np.flatnonzero(np.repeat(g < 0, C)), np.flatnonzero(np.repeat(g > 0, C))
    e = anywhere(rng)
    k = np.concatenate([rng.permutation(C) % 3 for r in range(N)])
    e[:, k == 0] = minus[e[:, k == 0] % (M // 2)]
    e[:, k == 1] = plus[e[:, k == 1] % (M // 2)]
    return {"x": x.astype(np.float32).astype(BF), "u": u.reshape(N, 128, 512), "v": d["v"], **still(rng), "sc": stored(e)}
def setup_inputs_one(rng):
    d = numbers_of(rng)
    x = d["x"].reshape(N, 128, C, 4)
    u = d["u"].reshape(N, 128, 128, 4)
    w = np.array(f(rng, N, 128, 2048)).reshape(N, 128, 4, 128, 4)
    for i, k in ((0, 2 ** 23), (127, -2 ** 23)):
        x[:, i] = 0
        x[:, i, :, 0] = 4
        u[:, i, 0] = 0
        u[:, i, 0, 0] = k
        w[:, i] = 0
        w[:, i, :, :, 0] = k
    for i in (0, 127):
        w[:, :, :, i] = 0
        w[:, i, 0, i, 0] = 32
    a = C * rng.permutation(N)
    e = a[0] + rng.integers(0, C, (4, M))
    e[:, a[1]:a[1] + C] = a[0] + rng.permutation(C)
    e[:, a[2]:a[2] + C] = e[:, a[2]:a[2] + 1].copy()
    c = a[0] + rng.permutation(C)
    e[:, c[:-1]] = np.roll(c[:-1], -1)
    e[:, c[-1]] = c[-1]
    return {"x": x.reshape(N, 128, 4 * C), "u": u.reshape(N, 128, 512), "v": d["v"], **weights(rng, w.reshape(N, 128, 2048)), "sc": stored(e)}
def setup_inputs_spread(rng):
    d = setup_inputs(rng)
    d["x"] = wide(rng, N, 128, 4 * C, cols=6)
    return d
def check_inputs(d):
    b = []
    for k in ("x", "u", "v"):
        a = np.abs(d[k].astype(np.float32))
        if not (np.isfinite(a).all() and ((a == 0) | (a >= 2.0 ** -30) & (a <= 2.0 ** 30)).all()): b.append("a value of " + k)
    if ((d["sc"] < 0) | (d["sc"] >= M)).any(): b.append("an entry of sc")
    return b
def reference(x, u, v, wc, ws, sc):
    qu = [mx_ref.quantize(u[r]) for r in range(N)]
    lay = [pk(wc[r], ws[r]) for r in range(N)]
    follow = np.concatenate([entries(sc[r]).reshape(4, C) for r in range(N)], axis=1)
    now = [x[r] for r in range(N)]
    for t in range(R):
        q = [mx_ref.quantize(now[r]) for r in range(N)]
        s = np.concatenate([mx_ref.matmul(qu[r], q[r])[0] for r in range(N)]) + np.float32(0.0)
        p = [follow[np.argmax(s[follow], axis=0), np.arange(M)]]
        for g in range(7): p.append(p[g][p[g]])
        p = np.stack(p)
        z = decode(join(*q)).astype(BF)
        z = decode(mx_ref.quantize(z)).astype(BF)
        now = []
        for r in range(N):
            h = mx_ref.quantize(gcols(z, p[:, C * r:C * r + C]))
            now.append(tile([np.maximum(mx_ref.matmul(pick(lay[r], np.arange(128 * b, 128 * b + 128)), h), np.float32(0.0)) * np.float32(0.03125) for b in range(4)]))
    y, pl = np.zeros((N, 128, C), np.float32), np.zeros((N, 8, C), np.float32)
    oc, osc = np.zeros((N, 128, 4 * C), np.uint8), np.zeros((N, 16, C), np.uint8)
    for r in range(N):
        last = mx_ref.quantize(now[r])
        y[r] = mx_ref.matmul(mx_ref.quantize(v[r]), last)
        pl[r] = p[:, C * r:C * r + C]
        oc[r], osc[r] = emit(last)
    return {"y": y, "pl": pl, "oc": oc, "osc": osc}

@@ -1,0 +1,489 @@
+from concourse.bass import DstId, RemoteDMATransfer
+from concourse.mybir import dt, AluOpType, ActivationFunctionType
+
+F32, BF, I32, U16, U8, X4 = "float32", "bfloat16", "int32", "uint16", "uint8", "float8_e4m3fn_x4"
+NS = 2048
+NAT = 7
+
+SCRATCH = {
+    "ps": ("psum", [128, 4096], F32),
+    "tab": ("sbuf", [128, 8 * NS], F32),
+    "win": ("sbuf", [128, 4 * NS], BF),
+    "ut": ("sbuf", [128, 512], BF), "vt": ("sbuf", [128, 512], BF),
+    "uq": ("sbuf", [128, 128], X4), "us": ("sbuf", [128, 128], U8),
+    "vq": ("sbuf", [128, 128], X4), "vs": ("sbuf", [128, 128], U8),
+    "wq": ("sbuf", [128, 512], X4), "wp": ("sbuf", [128, 512], U8),
+    "cb": ("sbuf", [128, 904], BF), "cb2": ("sbuf", [128, 520], BF),
+    "io1": ("sbuf", [128, 224], F32), "io2": ("sbuf", [128, 128], F32),
+    "rq": ("sbuf", [128, 896], X4), "rs": ("sbuf", [128, 896], U8),
+    "bq": ("sbuf", [128, 2048], X4), "bs": ("sbuf", [128, 2048], U8),
+    "sa": ("sbuf", [128, 24], I32), "sb": ("sbuf", [128, 56], I32),
+    "eb": ("sbuf", [128, 40], I32), "st": ("sbuf", [128, 16], U16),
+    "lc": ("sbuf", [128, 128], U16), "rc": ("sbuf", [128, 128], U16),
+    "offs": ("sbuf", [128, 64], U16), "ei": ("sbuf", [128, 128], I32),
+    "a0": ("sbuf", [128, 64], F32), "a1": ("sbuf", [128, 64], F32), "b0": ("sbuf", [128, 32], F32),
+    "mm": ("sbuf", [128, 32], F32), "w1": ("sbuf", [128, 64], F32),
+    "sg": ("sbuf", [128, 1024], F32), "tr": ("sbuf", [128, 1024], F32),
+    "rin": ("sbuf", [128, 256], F32), "rows": ("sbuf", [128, 8 * 256], F32), "trs": ("sbuf", [128, 512], F32),
+    "off": ("sbuf", [128, 64], U16), "offf": ("sbuf", [128, 16], U16),
+    "pi": ("sbuf", [128, 96], I32), "pko": ("sbuf", [128, 16], U16),
+    "tau": ("sbuf", [128, 8], F32),
+    "srow": ("sbuf", [128, 256], F32), "prow": ("sbuf", [128, 256], F32), "yt": ("sbuf", [128, 256], F32),
+    "dpo": ("dram", [4, 128, 4], F32), "dpi": ("dram", [4, 128, 4], F32),
+}
+for _t in range(3):
+    SCRATCH["x%d" % _t] = ("sbuf", [128, 1024], BF)
+    SCRATCH["xq%d" % _t] = ("sbuf", [128, 256], X4)
+    SCRATCH["xs%d" % _t] = ("sbuf", [128, 256], U8)
+for _t in range(2):
+    SCRATCH["ds%d" % _t] = ("dram", [8, 128, 2], F32)
+    SCRATCH["tl%d" % _t] = ("sbuf", [128, 1024], BF)
+    SCRATCH["tq%d" % _t] = ("sbuf", [128, 256], X4)
+    SCRATCH["ts%d" % _t] = ("sbuf", [128, 256], U8)
+    SCRATCH["lq%d" % _t] = ("sbuf", [128, 512], X4)
+    SCRATCH["ls%d" % _t] = ("sbuf", [128, 512], U8)
+    SCRATCH["gt%d" % _t] = ("sbuf", [128, 1024], BF)
+    SCRATCH["gq%d" % _t] = ("sbuf", [128, 512], X4)
+    SCRATCH["gs%d" % _t] = ("sbuf", [128, 512], U8)
+    SCRATCH["pq%d" % _t] = ("sbuf", [128, 256], X4)
+    SCRATCH["pp%d" % _t] = ("sbuf", [128, 256], U8)
+    SCRATCH["ht%d" % _t] = ("sbuf", [128, 1024], BF)
+    SCRATCH["hq%d" % _t] = ("sbuf", [128, 256], X4)
+    SCRATCH["hs%d" % _t] = ("sbuf", [128, 256], U8)
+
+SEMAPHORES = (["cV", "cS", "cP", "cG", "sent", "ldx", "ldu", "lda", "ldb", "ldw", "ldv", "stg", "own", "dpl", "outs",
+               "aC", "aP"] + ["tb%d" % k for k in range(7)]
+              + ["aS0", "aS1", "aT0", "aT1", "aX0", "aX1"])
+
+MAIN = [(1, 0), (1, 1), (1, 0), (1, 1), (3, 0), (3, 1), (5, 0), (5, 1), (11, 0), (11, 1)]
+PLAN = {0: (0, 1, [(0, 1)]),
+        1: (2, 1, [(1, 1), (1, 3), (1, 3)]),
+        2: (6, 11, [(1, 5), (1, 5), (3, 11)]),
+        3: (10, 43, [(5, 21), (5, 21), (11, 43)])}
+SLOT = {1: 1, 3: 2, 5: 3, 11: 4, 21: 5, 43: 6, 0: 2}
+
+
+def masks(topo, src, dsts, flip=False):
+    far = [d for d in dsts if topo.chip(d) != topo.chip(src)]
+    near = [d for d in dsts if topo.chip(d) == topo.chip(src)]
+    out, used = {}, []
+    for group in (far, near):
+        if not group:
+            continue
+        eng = [e for e in topo.engines(src, group[0]) if e not in used]
+        if group is far:
+            used = list(eng)
+        if flip:
+            eng = eng[::-1]
+        n = [1] * len(group)
+        grown = True
+        while grown:
+            grown = False
+            for i in range(len(group)):
+                if n[i] == min(n) and sum(n) + n[i] <= len(eng):
+                    n[i] *= 2
+                    grown = True
+        k = 0
+        for d, c in zip(group, n):
+            out[d] = eng[k:k + c]
+            k += c
+    return out
+
+
+def rank_program(g, core, T, topo):
+    r = T.rank_of(core)
+    if r is None:
+        return
+    N = len(T.cores)
+    a, h = r % 4, r // 4
+    Q = {"V": g.vector, "S": g.scalar, "P": g.tensor, "Y": g.sync, "G": g}
+    V, S, P = g.vector, g.scalar, g.tensor
+    A, ACT = AluOpType, ActivationFunctionType
+    count = {s: 0 for s in SEMAPHORES}
+    waited = {q: {} for q in Q}
+    acc = {}
+
+    def wait(q, tok):
+        if waited[q].get(tok[0], 0) < tok[1]:
+            Q[q].wait_ge(T.sem[tok[0]], tok[1])
+            waited[q][tok[0]] = tok[1]
+
+    def need(q, reads, writes):
+        want = {}
+        for (b, lo, hi), w in [(x, False) for x in reads] + [(x, True) for x in writes]:
+            for l2, h2, w2, tok in acc.get(b, []):
+                if l2 < hi and lo < h2 and (w or w2):
+                    want[tok[0]] = max(want.get(tok[0], 0), tok[1])
+        for s in want:
+            wait(q, (s, want[s]))
+
+    def note(reads, writes, tok):
+        for b, lo, hi in writes:
+            acc[b] = [e for e in acc.get(b, []) if not (lo <= e[0] and e[1] <= hi)] + [(lo, hi, True, tok)]
+        for b, lo, hi in reads:
+            acc.setdefault(b, []).append((lo, hi, False, tok))
+
+    def op(q, call, reads, writes):
+        ex = [x for x in reads if x[0] == "ps"]
+        reads = [x for x in reads if x[0] != "ps"]
+        writes = list(writes) + ex
+        need(q, reads, writes)
+        s = "c" + q
+        count[s] += 1
+        call().then_inc(T.sem[s], 1)
+        note(reads, writes, (s, count[s]))
+
+    def dmas(sem, items, reads, writes):
+        for q in sorted({it[0] for it in items}):
+            need(q, reads, writes)
+            if count[sem]:
+                wait(q, (sem, count[sem]))
+        for q, o, i in items:
+            Q[q].dma_start(o, i).then_inc(T.sem[sem], 16)
+            count[sem] += 16
+        note(reads, writes, (sem, count[sem]))
+
+    def send(sem, peers, src_of, dst_of, reads, flip=False):
+        need("G", reads, [])
+        m = masks(topo, core, [T.cores[d] for d in peers(r)], flip)
+        tr = []
+        for d in peers(r):
+            rid, pid, _ = topo.addr(T.cores[d])
+            tr.append(RemoteDMATransfer(dst_ids=[DstId(rid=rid, pnc=pid)], dma_engine_mask=sum(1 << e for e in m[T.cores[d]]),
+                                        remote_sem=T.sem[sem], src=src_of(d), dst=dst_of(d)))
+            count["sent"] += len(m[T.cores[d]])
+        g.remote_dma_fused(tr, local_sem=T.sem.sent)
+        for s in range(N):
+            if r in peers(s):
+                count[sem] += len(masks(topo, T.cores[s], [T.cores[d] for d in peers(s)], flip)[core])
+
+    def arrive(sem, writes):
+        for b, lo, hi in writes:
+            acc.setdefault(b, []).append((lo, hi, True, (sem, count[sem])))
+
+    def everyone(s):
+        return [(s + k) % N for k in range(1, N)]
+
+    def served(s):
+        return [4 * (s // 4) + (s + k) % 4 for k in range(1, 4)]
+
+    def bank(k):
+        return ("ps", 512 * k, 512 * k + 512)
+
+    def quant(qn, sn, c0, n, src, s0):
+        op("V", lambda: V.quantize_mx(T[qn][:, c0:c0 + n], T[sn][:, c0:c0 + n], T[src][:, s0:s0 + 4 * n]),
+           [(src, s0, s0 + 4 * n)], [(qn, c0, c0 + n), (sn, c0, c0 + n)])
+
+    def mx(k, lq, ls, l0, mq, ms, m0, n):
+        op("P", lambda: P.matmul_mx(T.ps[:, 512 * k:512 * k + n], T[lq][:, l0:l0 + 128], T[ls][:, l0:l0 + 128],
+                                    T[mq][:, m0:m0 + n], T[ms][:, m0:m0 + n], True, True),
+           [(lq, l0, l0 + 128), (ls, l0, l0 + 128), (mq, m0, m0 + n), (ms, m0, m0 + n)], [bank(k)])
+
+    def copy(q, o, i, reads, writes):
+        if q == "V":
+            op("V", lambda: V.tensor_copy(o, i), reads, writes)
+        else:
+            op("S", lambda: S.activation(o, i, ACT.Copy), reads, writes)
+
+    def ts(o, i, s1, o1, reads, writes, s2=None, o2=None):
+        if o2 is None:
+            op("V", lambda: V.tensor_scalar(o, i, s1, None, o1), reads, writes)
+        else:
+            op("V", lambda: V.tensor_scalar(o, i, s1, s2, o1, o2), reads, writes)
+
+    def tt(o, i0, i1, o1, reads, writes):
+        op("V", lambda: V.tensor_tensor(o, i0, i1, o1), reads, writes)
+
+    def fill(name, lo, hi, c):
+        op("V", lambda: V.memset(T[name][:, lo:hi], c), [], [(name, lo, hi)])
+
+    def iota(name, lo, hi, pattern, base, cm, flt=True):
+        if flt:
+            op("G", lambda: g.iota(T[name][:, lo:hi], pattern, base, cm, allow_small_or_imprecise_dtypes=True), [], [(name, lo, hi)])
+        else:
+            op("G", lambda: g.iota(T[name][:, lo:hi], pattern, base, cm), [], [(name, lo, hi)])
+
+    def codes(name, lo, hi):
+        return T[name][:, lo:hi].bitcast(dt.uint8)
+
+    dmas("ldx", [("Y", T.x0[:], T.x[:])], [], [("x0", 0, 1024)])
+    dmas("ldu", [("S", T.ut[:], T.u[:])], [], [("ut", 0, 512)])
+    dmas("lda", [("Y", T.sa[16 * G:16 * G + 16, 0:20], T.sc[:, 32 * (G % 2) + 4 * (G // 2):32 * (G % 2) + 4 * (G // 2) + 20])
+                 for G in range(8)], [], [("sa", 0, 24)])
+    dmas("ldb", [("S", T.sb[16 * G:16 * G + 16, 0:51], T.sc[:, G % 2 + 4 * (G // 2):G % 2 + 4 * (G // 2) + 51])
+                 for G in range(8)], [], [("sb", 0, 56)])
+    dmas("ldw", [("S", codes("wq", 0, 512), T.wc[:]), ("S", T.wp[:], T.ws[:])], [], [("wq", 0, 512), ("wp", 0, 512)])
+    dmas("ldv", [("S", T.vt[:], T.v[:])], [], [("vt", 0, 512)])
+
+    iota("io1", 0, 128, [[-1, 128]], 0, 1)
+    iota("io1", 128, 224, [[-1, 96]], 0, 1)
+    iota("io2", 0, 128, [[0, 4], [-1, 32]], 0, 1)
+    iota("pi", 0, 16, [[-32, 4], [0, 4]], 128, 1, False)
+    iota("pi", 16, 32, [[0, 16]], 0, 1, False)
+    iota("pi", 32, 48, [[0, 4], [16, 4]], 0, 0, False)
+    fill("cb", 0, 904, 0.0)
+    fill("cb2", 0, 520, 0.0)
+    fill("a0", 0, 64, 0.0)
+    fill("b0", 0, 32, 0.0)
+    fill("rin", 0, 256, 0.0)
+    ts(T.cb[:, 3:899:4], T.io1[:], 0.0, A.is_equal, [("io1", 0, 224)], [("cb", 0, 904)])
+    for b in range(4):
+        quant("rq", "rs", 224 * b, 224, "cb", 3 - b)
+
+    def spread_tiles(q):
+        ts(T.cb2[:, 3:515:4], T.io2[:], float(32 * q), A.is_equal, [("io2", 0, 128)], [("cb2", 0, 520)])
+        for b in range(4):
+            quant("bq", "bs", 128 * (4 * q + b), 128, "cb2", 3 - b)
+
+    def init_slot(k):
+        for u in range(2):
+            lo = NS * k + 1024 * u
+            copy("S", T.tab[:, lo:lo + 1024], T.x0[:], [("x0", 0, 1024)], [("tab", lo, lo + 1024)])
+
+    def table(k, src_of, reads, queues):
+        dmas("tb%d" % k, [(queues[G % len(queues)], T.tab[16 * G:16 * G + 1, NS * k:NS * k + NS], src_of) for G in range(8)],
+             reads, [("tab", NS * k, NS * k + NS)])
+
+    nmain, xb, branch = PLAN[a]
+    slots = [0, 1] + [SLOT[p] for p in (3, 5, 11, 21, 43) if any(p in st for st in branch) or any(p == m[0] for m in MAIN[:nmain])]
+
+    for t in range(2):
+        X, xq, xs, ds = "x%d" % t, "xq%d" % t, "xs%d" % t, "ds%d" % t
+        tl, tq, tsc, lq, ls = "tl%d" % t, "tq%d" % t, "ts%d" % t, "lq%d" % t, "ls%d" % t
+        gt, gq, gs, pq, pp = "gt%d" % t, "gq%d" % t, "gs%d" % t, "pq%d" % t, "pp%d" % t
+        ht, hq, hs = "ht%d" % t, "hq%d" % t, "hs%d" % t
+
+        if t == 0:
+            quant("uq", "us", 0, 128, "ut", 0)
+        quant(xq, xs, 0, 256, X, 0)
+        mx(7, "uq", "us", 0, xq, xs, 0, 256)
+        copy("V", T.srow[0:1, :], T.ps[0:1, 512 * 7:512 * 7 + 256], [bank(7)], [("srow", 0, 256)])
+        dmas("stg", [("Y", T[ds][r], T.srow[0:1, :])], [("srow", 0, 256)], [(ds, r, r + 1)])
+        send("aS%d" % t, everyone, lambda d: T[ds][r], lambda d: T[ds][r], [(ds, r, r + 1)])
+        arrive("aS%d" % t, [(ds, 0, N)])
+
+        if t == 0:
+            for k in slots:
+                if k <= 4:
+                    init_slot(k)
+            for k1 in range(2):
+                for b0 in range(2):
+                    copy("V", T.st[:, 8 * b0 + 2 * k1:8 * b0 + 2 * k1 + 2], T.sa[:, 16 * k1 + 2 * b0:16 * k1 + 2 * b0 + 2],
+                         [("sa", 0, 24)], [("st", 8 * b0 + 2 * k1, 8 * b0 + 2 * k1 + 2)])
+            for b0 in range(2):
+                copy("V", T.eb[:, 4 * b0:4 * b0 + 4], T.sb[:, 2 * b0:2 * b0 + 49:16], [("sb", 0, 56)], [("eb", 4 * b0, 4 * b0 + 4)])
+            e = lambda k: T.eb[:, 8 * k:8 * k + 8]
+            er = lambda k: ("eb", 8 * k, 8 * k + 8)
+            ts(e(1), e(0), 6, A.logical_shift_right, [er(0)], [er(1)], 3, A.bitwise_and)
+            ts(e(2), e(0), 8, A.logical_shift_right, [er(0)], [er(2)])
+            ts(e(3), e(0), 63, A.bitwise_and, [er(0)], [er(3)])
+            ts(e(1), e(1), 512.0, A.mult, [er(1)], [er(1)])
+            ts(e(2), e(2), 64.0, A.mult, [er(2)], [er(2)])
+            tt(e(3), e(3), e(1), A.add, [er(1), er(3)], [er(3)])
+            tt(e(3), e(3), e(2), A.add, [er(2), er(3)], [er(3)])
+            for b0 in range(2):
+                copy("V", T.st[:, 8 * b0 + 4:8 * b0 + 8], T.eb[:, 24 + 4 * b0:28 + 4 * b0], [er(3)], [("st", 8 * b0 + 4, 8 * b0 + 8)])
+            send("aC", everyone, lambda d: T.st[:], lambda d: T.lc[:, 16 * r:16 * r + 16], [("st", 0, 16)])
+            copy("V", T.lc[:, 16 * r:16 * r + 16], T.st[:], [("st", 0, 16)], [("lc", 16 * r, 16 * r + 16)])
+            arrive("aC", [("lc", 0, 128)])
+
+        n = 0
+        for c in range(4):
+            for q in range(4):
+                blk = (q - c) % 4
+                eng = "S" if t == 1 and n % 3 == 2 else "V"
+                n += 1
+                lo = 256 * c + q
+                copy(eng, T[tl][32 * q:32 * q + 32, 256 * c:256 * c + 256], T[X][32 * c:32 * c + 32, 256 * blk:256 * blk + 256],
+                     [(X, 0, 1024)], [(tl, lo, lo + 1)])
+        quant(tq, tsc, 0, 256, tl, 0)
+        send("aT%d" % t, everyone, lambda d: codes(tq, 64 * (d % 4), 64 * (d % 4) + 64), lambda d: codes(lq, 64 * r, 64 * r + 64),
+             [(tq, 0, 256)])
+        send("aT%d" % t, everyone, lambda d: T[tsc][:, 64 * (d % 4):64 * (d % 4) + 64], lambda d: T[ls][:, 64 * r:64 * r + 64],
+             [(tsc, 0, 256)], True)
+
+        table(0, T[ds][:], [(ds, 0, N)], "Y" if t == 0 else "YS")
+        dmas("own", [("Y", codes(lq, 64 * r, 64 * r + 64), codes(tq, 64 * a, 64 * a + 64)),
+                     ("Y", T[ls][:, 64 * r:64 * r + 64], T[tsc][:, 64 * a:64 * a + 64])],
+             [(tq, 0, 256), (tsc, 0, 256)], [(lq, 64 * r, 64 * r + 64), (ls, 64 * r, 64 * r + 64)])
+        arrive("aT%d" % t, [(lq, 0, 512), (ls, 0, 512)])
+
+        if t == 0:
+            for k in slots:
+                if k > 4:
+                    iota("tab", NS * k, NS * k + NS, [[0, NS]], 0, 0)
+            if a == 0:
+                iota("tab", NS * SLOT[0], NS * SLOT[0] + NS, [[1, NS]], 0, 0)
+            for q in range(4):
+                spread_tiles(q)
+            rc = "lc"
+            if a:
+                rc = "rc"
+                for q in range(4):
+                    q2 = (q + a) % 4
+                    copy("V", T.rc[32 * q2:32 * q2 + 32, :], T.lc[32 * q:32 * q + 32, :], [("lc", 0, 128)], [("rc", q, q + 1)])
+            for k1 in range(2):
+                for hh in range(2):
+                    for u in range(2):
+                        o, i = 32 * k1 + 2 * hh + u, 64 * hh + 2 * k1 + u
+                        copy("V", T.offs[:, o:32 * k1 + 32:4], T[rc][:, i:64 * hh + 64:8], [(rc, 0, 128)], [("offs", o, o + 1)])
+        else:
+            for q in range(4):
+                lo = NS * NAT + 512 * q
+                iota("tab", lo, lo + 512, [[256, 8], [1, 64]], 64 * ((q - a) % 4), 0)
+
+        def score_gather(q, k):
+            copy(q, T.sg[:, 256 * k:256 * k + 256], T.tab[:, 0:NS].indirect(T.offs[:, 16 * k:16 * k + 16]),
+                 [("tab", 0, NS), ("offs", 0, 64)], [("sg", 256 * k, 256 * k + 256)])
+        for k in range(4):
+            score_gather("V" if t == 1 and k == 0 else "S", k)
+        if t == 0:
+            for k1 in range(2):
+                for hh in range(2):
+                    for x in range(2):
+                        o, i = 32 * k1 + 2 * hh + x, 64 * hh + 4 + 2 * x + k1
+                        ts(T.ei[:, o:32 * k1 + 32:4], T[rc][:, i:64 * hh + 64:8], float(512 * a), A.add, [(rc, 0, 128)], [("ei", o, o + 1)])
+            ts(T.ei[:, 64:128], T.ei[:, 0:64], NS - 1, A.bitwise_and, [("ei", 0, 64)], [("ei", 64, 128)])
+            tt(T.a1[:, 0:64:2], T.ei[:, 96:128], T.ei[:, 64:96], A.subtract, [("ei", 64, 128)], [("a1", 0, 1)])
+            copy("V", T.a1[:, 1:64:2], T.ei[:, 64:96], [("ei", 64, 128)], [("a1", 1, 2)])
+        for k in range(4):
+            op("V", lambda: V.transpose(T.tr[:, 256 * k:256 * k + 256], T.sg[:, 256 * k:256 * k + 256]),
+               [("sg", 256 * k, 256 * k + 256)], [("tr", 256 * k, 256 * k + 256)])
+        tt(T.a0[:, 1:64:2], T.tr[:, 512:1024:16], T.tr[:, 0:512:16], A.is_gt, [("tr", 0, 1024)], [("a0", 0, 64)])
+        tt(T.mm[:], T.tr[:, 512:1024:16], T.tr[:, 0:512:16], A.max, [("tr", 0, 1024)], [("mm", 0, 32)])
+        op("V", lambda: V.tensor_tensor_scan(T.w1[:], T.a0[:], T.a1[:], 0.0, A.mult, A.add),
+           [("a0", 0, 64), ("a1", 0, 64)], [("w1", 0, 64)])
+        tt(T.b0[:, 1:32:2], T.mm[:, 0:32:2], T.mm[:, 1:32:2], A.is_ge, [("mm", 0, 32)], [("b0", 0, 32)])
+        tt(T.w1[:, 1:64:4], T.w1[:, 1:64:4], T.w1[:, 3:64:4], A.subtract, [("w1", 0, 64)], [("w1", 0, 64)])
+        op("V", lambda: V.tensor_tensor_scan(T.rin[:, 0:256:8], T.b0[:], T.w1[:, 1:64:2], 0.0, A.mult, A.add),
+           [("b0", 0, 32), ("w1", 0, 64)], [("rin", 0, 256)])
+        op("V", lambda: V.transpose(T.rows[:, 256:512], T.rin[:]), [("rin", 0, 256)], [("rows", 256, 512)])
+        table(1, T.rows[8:128:16, 256:512], [("rows", 256, 512)], "YS")
+
+        if t == 0:
+            p = lambda k: T.pi[:, 16 * k:16 * k + 16]
+            pr = lambda k: ("pi", 16 * k, 16 * k + 16)
+            ts(p(0), p(0), 5, A.logical_shift_right, [pr(0)], [pr(0)], 3, A.bitwise_and)
+            ts(p(5), p(1), 4, A.logical_shift_right, [pr(1)], [pr(5)], 1, A.bitwise_and)
+            ts(p(1), p(1), 15, A.bitwise_and, [pr(1)], [pr(1)])
+            ts(p(3), p(0), float(a), A.is_equal, [pr(0)], [pr(3)], -256.0, A.mult)
+            ts(p(4), p(0), 64.0, A.mult, [pr(0)], [pr(4)], 256.0, A.add)
+            tt(p(1), p(1), p(2), A.add, [pr(1), pr(2)], [pr(1)])
+            tt(p(3), p(3), p(4), A.add, [pr(3), pr(4)], [pr(3)])
+            tt(p(3), p(3), p(1), A.add, [pr(3), pr(1)], [pr(3)])
+            copy("V", T.pko[:], p(3), [pr(3)], [("pko", 0, 16)])
+            if len(branch) > 1:
+                s0, s1 = SLOT[branch[1][0]], SLOT[branch[1][1]]
+                lo = min(s0, s1)
+                ts(T.tau[:, 0:1], T.pi[:, 80:81], float(NS * (s1 - s0)), A.mult, [pr(5)], [("tau", 0, 1)], float(NS * (s0 - lo)), A.add)
+            quant("vq", "vs", 0, 128, "vt", 0)
+
+        n = 0
+        for q in range(4):
+            for b in range(4):
+                mx(n % 4, "bq", "bs", 128 * (4 * q + b), lq, ls, 0, 512)
+                lo = NS * b + 512 * q
+                copy("S", T.win[:, lo:lo + 512], T.ps[:, 512 * (n % 4):512 * (n % 4) + 512], [bank(n % 4)], [("win", lo, lo + 512)])
+                n += 1
+
+        turn = [0]
+
+        def step(offc, lo, hi, row):
+            copy("V", T.rows[:, 256 * row:256 * row + 256], T.tab[:, NS * lo:NS * hi].indirect(T.off[:, offc:offc + 16]),
+                 [("tab", NS * lo, NS * hi), ("off", offc, offc + 16)], [("rows", 256 * row, 256 * row + 256)])
+
+        def turn_row(row):
+            c = 256 * (turn[0] % 2)
+            turn[0] += 1
+            op("V", lambda: V.transpose(T.trs[:, c:c + 256], T.rows[:, 256 * row:256 * row + 256]),
+               [("rows", 256 * row, 256 * row + 256)], [("trs", c, c + 256)])
+            return ("trs", c)
+
+        cur, power, oc = ("rin", 8), 1, 0
+        for tb, make in MAIN[:nmain]:
+            copy("V", T.off[:, oc:oc + 16], T[cur[0]][:, cur[1]:cur[1] // 256 * 256 + 256:16],
+                 [(cur[0], cur[1], cur[1] + 248)], [("off", oc, oc + 16)])
+            power += tb
+            row = SLOT[power] if make else 0
+            step(oc, SLOT[tb], SLOT[tb] + 1, row)
+            if make:
+                table(row, T.rows[0:128:16, 256 * row:256 * row + 256], [("rows", 256 * row, 256 * row + 256)], "Y")
+            if power < xb or power == xb:
+                cur = turn_row(row)
+            elif tb != MAIN[nmain - 1][0] or not make:
+                cur = turn_row(row)
+            oc = 16 - oc
+        if xb == 1:
+            cur = ("rin", 8)
+        for k, (p0, p1) in enumerate(branch):
+            s0, s1 = SLOT[p0], SLOT[p1]
+            lo, hi = min(s0, s1), max(s0, s1) + 1
+            end = cur[1] // 256 * 256 + 256
+            rd = [(cur[0], cur[1], cur[1] + 248)]
+            if k % 2 == 0:
+                for u, s in ((0, s0), (1, s1)):
+                    c = cur[1] + 16 * (h if k == 0 else u)
+                    ts(T.off[:, oc + u:oc + 16:2], T[cur[0]][:, c:end:32], float(NS * (s - lo)), A.add, rd, [("off", oc + u, oc + u + 1)])
+            else:
+                ts(T.off[:, oc:oc + 16], T[cur[0]][:, cur[1]:end:16], T.tau[:, 0:1], A.add, rd + [("tau", 0, 1)], [("off", oc, oc + 16)])
+            step(oc, lo, hi, 0 if k % 2 else 7)
+            cur = turn_row(0 if k % 2 else 7)
+            oc = 16 - oc
+        copy("V", T.offf[:], T.trs[:, cur[1]:cur[1] + 256:16], [("trs", cur[1], cur[1] + 256)], [("offf", 0, 16)])
+
+        for b in range(4):
+            copy("VS"[b % 2], T[gt][:, b:1024:4], T.win[:, NS * b:NS * b + NS].indirect(T.offf[:]),
+                 [("win", NS * b, NS * b + NS), ("offf", 0, 16)], [(gt, b, b + 1)])
+        quant(gq, gs, 0, 256, gt, 0)
+        send("aX%d" % t, served, lambda d: codes(gq, 64 * (d % 4), 64 * (d % 4) + 64),
+             lambda d: codes(gq, 256 + 64 * a, 320 + 64 * a), [(gq, 0, 256)])
+        send("aX%d" % t, served, lambda d: T[gs][:, 64 * (d % 4):64 * (d % 4) + 64],
+             lambda d: T[gs][:, 256 + 64 * a:320 + 64 * a], [(gs, 0, 256)])
+        arrive("aX%d" % t, [(gq, 256, 512), (gs, 256, 512)])
+
+        if t == 1:
+            copy("V", T.prow[:], T.tab[:, NS * NAT:NS * NAT + NS].indirect(T.offf[:]),
+                 [("tab", NS * NAT, NS * NAT + NS), ("offf", 0, 16)], [("prow", 0, 256)])
+            dmas("dpl", [("Y", T.dpo[d % 4], T.prow[0:128:16, 64 * (d % 4):64 * (d % 4) + 64]) for d in served(r)],
+                 [("prow", 0, 256)], [("dpo", 0, 4)])
+            send("aP", served, lambda d: T.dpo[d % 4], lambda d: T.dpi[a], [("dpo", 0, 4)])
+            arrive("aP", [("dpi", 0, 4)])
+            outs = [("Y", T.pl[2 * a:2 * a + 2, 64 * ((q - a) % 4):64 * ((q - a) % 4) + 64],
+                     T.prow[32 * q:32 * q + 32:16, 64 * a:64 * a + 64]) for q in range(4)]
+            dmas("own", outs, [("prow", 0, 256)], [])
+            outs = [("Y", T.pl[2 * c:2 * c + 2, 64 * ((q - c) % 4):64 * ((q - c) % 4) + 64], T.dpi[c, 32 * q:32 * q + 32, :])
+                    for c in range(4) if c != a for q in range(4)]
+            dmas("stg", outs, [("dpi", 0, 4)], [])
+
+        op("V", lambda: V.tensor_copy(T[pq][:].bitcast(dt.uint32), T[gq][:, 0:512].bitcast(dt.uint32).indirect(T.pko[:])),
+           [(gq, 0, 512), ("pko", 0, 16)], [(pq, 0, 256)])
+        copy("S", T[pp][:], T[gs][:, 0:512].indirect(T.pko[:]), [(gs, 0, 512), ("pko", 0, 16)], [(pp, 0, 256)])
+        n = 0
+        for k in range(4):
+            for b in range(4):
+                m0 = min(64 * k, 128)
+                mx(n % 8, "rq", "rs", 224 * b + 32 * k, pq, pp, m0, 128)
+                c = 512 * (n % 8) + 64 * k - m0
+                lo = 256 * k + b
+                copy("VS"[n % 2], T[ht][:, lo:256 * k + 256:4], T.ps[:, c:c + 64], [bank(n % 8)], [(ht, lo, lo + 1)])
+                n += 1
+        quant(hq, hs, 0, 256, ht, 0)
+        Xn = "x%d" % (t + 1)
+        for b in range(4):
+            mx(b, "wq", "wp", 128 * b, hq, hs, 0, 256)
+            o, i = T[Xn][:, b:1024:4], T.ps[:, 512 * b:512 * b + 256]
+            if b % 2 == 0:
+                op("S", lambda: S.activation(o, i, ACT.Relu, scale=0.03125), [bank(b)], [(Xn, b, b + 1)])
+            else:
+                ts(o, i, 0.0, A.max, [bank(b)], [(Xn, b, b + 1)], 0.03125, A.mult)
+
+    quant("xq2", "xs2", 0, 256, "x2", 0)
+    mx(7, "vq", "vs", 0, "xq2", "xs2", 0, 256)
+    dmas("outs", [("S", T.oc[:], codes("xq2", 0, 256))]
+         + [("S", T.osc[4 * k:4 * k + 4, :], T.xs2[32 * k:32 * k + 4, :]) for k in range(4)],
+         [("xq2", 0, 256), ("xs2", 0, 256)], [])
+    copy("V", T.yt[:], T.ps[:, 512 * 7:512 * 7 + 256], [bank(7)], [("yt", 0, 256)])
+    dmas("ldx", [("Y", T.y[:], T.yt[:])], [("yt", 0, 256)], [])
+    for s in SEMAPHORES:
+        if count[s]:
+            wait("G", (s, count[s]))

@@ -24,7 +24,7 @@ SCRATCH = {
     "a0": ("sbuf", [128, 64], F32), "a1": ("sbuf", [128, 64], F32), "b0": ("sbuf", [128, 32], F32),
     "mm": ("sbuf", [128, 32], F32), "w1": ("sbuf", [128, 64], F32),
     "sg": ("sbuf", [128, 1024], F32), "tr": ("sbuf", [128, 1024], F32),
-    "rin": ("sbuf", [128, 256], F32), "rows": ("sbuf", [128, 8 * 256], F32), "trs": ("sbuf", [128, 512], F32),
+    "rin": ("sbuf", [128, 256], F32), "rows": ("sbuf", [128, 9 * 256], F32), "trs": ("sbuf", [128, 512], F32),
     "off": ("sbuf", [128, 64], U16), "offf": ("sbuf", [128, 16], U16),
     "pi": ("sbuf", [128, 96], I32), "pko": ("sbuf", [128, 16], U16),
     "tau": ("sbuf", [128, 8], F32),
@@ -40,6 +40,8 @@ for _t in range(2):
     SCRATCH["tl%d" % _t] = ("sbuf", [128, 1024], BF)
     SCRATCH["tq%d" % _t] = ("sbuf", [128, 256], X4)
     SCRATCH["ts%d" % _t] = ("sbuf", [128, 256], U8)
+    SCRATCH["fq%d" % _t] = ("sbuf", [128, 256], X4)
+    SCRATCH["fs%d" % _t] = ("sbuf", [128, 256], U8)
     SCRATCH["lq%d" % _t] = ("sbuf", [128, 512], X4)
     SCRATCH["ls%d" % _t] = ("sbuf", [128, 512], U8)
     SCRATCH["gt%d" % _t] = ("sbuf", [128, 1024], BF)
@@ -53,7 +55,7 @@ for _t in range(2):
 
 SEMAPHORES = (["cV", "cS", "cP", "cG", "sent", "ldx", "ldu", "lda", "ldb", "ldw", "ldv", "stg", "own", "dpl", "outs",
                "aC", "aP"] + ["tb%d" % k for k in range(7)]
-              + ["aS0", "aS1", "aT0", "aT1", "aX0", "aX1"])
+              + ["aS0", "aS1", "aT0", "aT1", "aX0", "aX1", "hq0", "hq1", "hs0", "hs1"])
 
 MAIN = [(1, 0), (1, 1), (1, 0), (1, 1), (3, 0), (3, 1), (5, 0), (5, 1), (11, 0), (11, 1)]
 PLAN = {0: (0, 1, [(0, 1)]),
@@ -61,9 +63,10 @@ PLAN = {0: (0, 1, [(0, 1)]),
         2: (6, 11, [(1, 5), (1, 5), (3, 11)]),
         3: (10, 43, [(5, 21), (5, 21), (11, 43)])}
 SLOT = {1: 1, 3: 2, 5: 3, 11: 4, 21: 5, 43: 6, 0: 2}
+HELPED = 6
 
 
-def masks(topo, src, dsts, flip=False):
+def masks(topo, src, dsts):
     far = [d for d in dsts if topo.chip(d) != topo.chip(src)]
     near = [d for d in dsts if topo.chip(d) == topo.chip(src)]
     out, used = {}, []
@@ -73,8 +76,6 @@ def masks(topo, src, dsts, flip=False):
         eng = [e for e in topo.engines(src, group[0]) if e not in used]
         if group is far:
             used = list(eng)
-        if flip:
-            eng = eng[::-1]
         n = [1] * len(group)
         grown = True
         while grown:
@@ -90,11 +91,50 @@ def masks(topo, src, dsts, flip=False):
     return out
 
 
+def helpers(topo, cores, c):
+    idle = [x for x in topo.cores_of(c) if x not in cores and topo.die(x) == topo.die(c)]
+    one = [x for x in idle if all(topo.may_write(x, d) for d in cores)][0]
+    two = [x for x in idle if x != one][0]
+    easy = [d for d in cores if d != c and topo.may_write(two, d)]
+    return {one: [d for d in cores if d != c and d not in easy], two: easy}
+
+
+def fused(g, T, topo, src, dsts, sem, src_of, dst_of):
+    m = masks(topo, src, dsts)
+    tr = []
+    for d in dsts:
+        rid, pid, _ = topo.addr(d)
+        tr.append(RemoteDMATransfer(dst_ids=[DstId(rid=rid, pnc=pid)], dma_engine_mask=sum(1 << e for e in m[d]),
+                                    remote_sem=T.sem[sem], src=src_of(d), dst=dst_of(d)))
+    g.remote_dma_fused(tr, local_sem=T.sem.sent)
+    return sum(len(m[d]) for d in dsts)
+
+
+def hand_on(g, core, T, topo):
+    cores = list(T.cores)
+    for s, c in enumerate(cores):
+        hp = helpers(topo, cores, c)
+        if core not in hp:
+            continue
+        n, sent = len(masks(topo, c, list(hp))[core]), 0
+        for t in range(2):
+            lo = lambda d: 64 * (cores.index(d) % 4)
+            g.wait_ge(T.sem["hq%d" % t], n)
+            sent += fused(g, T, topo, core, hp[core], "aT%d" % t, lambda d: T["fq%d" % t][:, lo(d):lo(d) + 64].bitcast(dt.uint8),
+                          lambda d: T["lq%d" % t][:, 64 * s:64 * s + 64].bitcast(dt.uint8))
+            g.wait_ge(T.sem["hs%d" % t], n)
+            sent += fused(g, T, topo, core, hp[core], "aT%d" % t, lambda d: T["fs%d" % t][:, lo(d):lo(d) + 64],
+                          lambda d: T["ls%d" % t][:, 64 * s:64 * s + 64])
+        g.wait_ge(T.sem.sent, sent)
+
+
 def rank_program(g, core, T, topo):
     r = T.rank_of(core)
     if r is None:
+        hand_on(g, core, T, topo)
         return
-    N = len(T.cores)
+    cores = list(T.cores)
+    N = len(cores)
     a, h = r % 4, r // 4
     Q = {"V": g.vector, "S": g.scalar, "P": g.tensor, "Y": g.sync, "G": g}
     V, S, P = g.vector, g.scalar, g.tensor
@@ -143,19 +183,13 @@ def rank_program(g, core, T, topo):
             count[sem] += 16
         note(reads, writes, (sem, count[sem]))
 
-    def send(sem, peers, src_of, dst_of, reads, flip=False):
+    def send(sem, peers, src_of, dst_of, reads):
         need("G", reads, [])
-        m = masks(topo, core, [T.cores[d] for d in peers(r)], flip)
-        tr = []
-        for d in peers(r):
-            rid, pid, _ = topo.addr(T.cores[d])
-            tr.append(RemoteDMATransfer(dst_ids=[DstId(rid=rid, pnc=pid)], dma_engine_mask=sum(1 << e for e in m[T.cores[d]]),
-                                        remote_sem=T.sem[sem], src=src_of(d), dst=dst_of(d)))
-            count["sent"] += len(m[T.cores[d]])
-        g.remote_dma_fused(tr, local_sem=T.sem.sent)
+        count["sent"] += fused(g, T, topo, core, [cores[d] for d in peers(r)], sem,
+                               lambda c: src_of(cores.index(c)), lambda c: dst_of(cores.index(c)))
         for s in range(N):
             if r in peers(s):
-                count[sem] += len(masks(topo, T.cores[s], [T.cores[d] for d in peers(s)], flip)[core])
+                count[sem] += len(masks(topo, cores[s], [cores[d] for d in peers(s)])[core])
 
     def arrive(sem, writes):
         for b, lo, hi in writes:
@@ -212,28 +246,28 @@ def rank_program(g, core, T, topo):
                  for G in range(8)], [], [("sa", 0, 24)])
     dmas("ldb", [("S", T.sb[16 * G:16 * G + 16, 0:51], T.sc[:, G % 2 + 4 * (G // 2):G % 2 + 4 * (G // 2) + 51])
                  for G in range(8)], [], [("sb", 0, 56)])
-    dmas("ldw", [("S", codes("wq", 0, 512), T.wc[:]), ("S", T.wp[:], T.ws[:])], [], [("wq", 0, 512), ("wp", 0, 512)])
-    dmas("ldv", [("S", T.vt[:], T.v[:])], [], [("vt", 0, 512)])
 
+    iota("io2", 0, 128, [[0, 4], [-1, 32]], 0, 1)
     iota("io1", 0, 128, [[-1, 128]], 0, 1)
     iota("io1", 128, 224, [[-1, 96]], 0, 1)
-    iota("io2", 0, 128, [[0, 4], [-1, 32]], 0, 1)
     iota("pi", 0, 16, [[-32, 4], [0, 4]], 128, 1, False)
     iota("pi", 16, 32, [[0, 16]], 0, 1, False)
     iota("pi", 32, 48, [[0, 4], [16, 4]], 0, 0, False)
-    fill("cb", 0, 904, 0.0)
     fill("cb2", 0, 520, 0.0)
     fill("a0", 0, 64, 0.0)
     fill("b0", 0, 32, 0.0)
     fill("rin", 0, 256, 0.0)
-    ts(T.cb[:, 3:899:4], T.io1[:], 0.0, A.is_equal, [("io1", 0, 224)], [("cb", 0, 904)])
-    for b in range(4):
-        quant("rq", "rs", 224 * b, 224, "cb", 3 - b)
 
     def spread_tiles(q):
         ts(T.cb2[:, 3:515:4], T.io2[:], float(32 * q), A.is_equal, [("io2", 0, 128)], [("cb2", 0, 520)])
         for b in range(4):
             quant("bq", "bs", 128 * (4 * q + b), 128, "cb2", 3 - b)
+
+    def unit_tiles():
+        fill("cb", 0, 904, 0.0)
+        ts(T.cb[:, 3:899:4], T.io1[:], 0.0, A.is_equal, [("io1", 0, 224)], [("cb", 0, 904)])
+        for b in range(4):
+            quant("rq", "rs", 224 * b, 224, "cb", 3 - b)
 
     def init_slot(k):
         for u in range(2):
@@ -244,8 +278,10 @@ def rank_program(g, core, T, topo):
         dmas("tb%d" % k, [(queues[G % len(queues)], T.tab[16 * G:16 * G + 1, NS * k:NS * k + NS], src_of) for G in range(8)],
              reads, [("tab", NS * k, NS * k + NS)])
 
+    spread_tiles(0)
     nmain, xb, branch = PLAN[a]
     slots = [0, 1] + [SLOT[p] for p in (3, 5, 11, 21, 43) if any(p in st for st in branch) or any(p == m[0] for m in MAIN[:nmain])]
+    mine = list(helpers(topo, cores, core))
 
     for t in range(2):
         X, xq, xs, ds = "x%d" % t, "xq%d" % t, "xs%d" % t, "ds%d" % t
@@ -263,8 +299,10 @@ def rank_program(g, core, T, topo):
         arrive("aS%d" % t, [(ds, 0, N)])
 
         if t == 0:
+            dmas("ldw", [("Y", codes("wq", 0, 512), T.wc[:]), ("Y", T.wp[:], T.ws[:])], [], [("wq", 0, 512), ("wp", 0, 512)])
+            dmas("ldv", [("Y", T.vt[:], T.v[:])], [], [("vt", 0, 512)])
             for k in slots:
-                if k <= 4:
+                if k <= 2:
                     init_slot(k)
             for k1 in range(2):
                 for b0 in range(2):
@@ -297,24 +335,30 @@ def rank_program(g, core, T, topo):
                 copy(eng, T[tl][32 * q:32 * q + 32, 256 * c:256 * c + 256], T[X][32 * c:32 * c + 32, 256 * blk:256 * blk + 256],
                      [(X, 0, 1024)], [(tl, lo, lo + 1)])
         quant(tq, tsc, 0, 256, tl, 0)
-        send("aT%d" % t, everyone, lambda d: codes(tq, 64 * (d % 4), 64 * (d % 4) + 64), lambda d: codes(lq, 64 * r, 64 * r + 64),
-             [(tq, 0, 256)])
-        send("aT%d" % t, everyone, lambda d: T[tsc][:, 64 * (d % 4):64 * (d % 4) + 64], lambda d: T[ls][:, 64 * r:64 * r + 64],
-             [(tsc, 0, 256)], True)
+        need("G", [(tq, 0, 256), (tsc, 0, 256)], [])
+        count["sent"] += fused(g, T, topo, core, mine, "hq%d" % t, lambda c: codes(tq, 0, 256), lambda c: codes("fq%d" % t, 0, 256))
+        count["sent"] += fused(g, T, topo, core, mine, "hs%d" % t, lambda c: T[tsc][:], lambda c: T["fs%d" % t][:])
+        for c in cores:
+            for hc, to in helpers(topo, cores, c).items():
+                if core in to:
+                    count["aT%d" % t] += 2 * len(masks(topo, hc, to)[core])
 
-        table(0, T[ds][:], [(ds, 0, N)], "Y" if t == 0 else "YS")
         dmas("own", [("Y", codes(lq, 64 * r, 64 * r + 64), codes(tq, 64 * a, 64 * a + 64)),
                      ("Y", T[ls][:, 64 * r:64 * r + 64], T[tsc][:, 64 * a:64 * a + 64])],
-             [(tq, 0, 256), (tsc, 0, 256)], [(lq, 64 * r, 64 * r + 64), (ls, 64 * r, 64 * r + 64)])
+             [(tq, 0, 256), (tsc, 0, 256)], [(lq, 64 * r, 64 * r + 64), (ls, 64 * r, 64 * r + 64)]) if t == 1 else None
+        table(0, T[ds][:], [(ds, 0, N)], "YS")
+        dmas("own", [("Y", codes(lq, 64 * r, 64 * r + 64), codes(tq, 64 * a, 64 * a + 64)),
+                     ("Y", T[ls][:, 64 * r:64 * r + 64], T[tsc][:, 64 * a:64 * a + 64])],
+             [(tq, 0, 256), (tsc, 0, 256)], [(lq, 64 * r, 64 * r + 64), (ls, 64 * r, 64 * r + 64)]) if t == 0 else None
         arrive("aT%d" % t, [(lq, 0, 512), (ls, 0, 512)])
 
         if t == 0:
             for k in slots:
-                if k > 4:
+                if k > 3:
                     iota("tab", NS * k, NS * k + NS, [[0, NS]], 0, 0)
             if a == 0:
                 iota("tab", NS * SLOT[0], NS * SLOT[0] + NS, [[1, NS]], 0, 0)
-            for q in range(4):
+            for q in range(1, 4):
                 spread_tiles(q)
             rc = "lc"
             if a:
@@ -333,8 +377,9 @@ def rank_program(g, core, T, topo):
                 iota("tab", lo, lo + 512, [[256, 8], [1, 64]], 64 * ((q - a) % 4), 0)
 
         def score_gather(q, k):
+            h0 = 32 * (k // 2)
             copy(q, T.sg[:, 256 * k:256 * k + 256], T.tab[:, 0:NS].indirect(T.offs[:, 16 * k:16 * k + 16]),
-                 [("tab", 0, NS), ("offs", 0, 64)], [("sg", 256 * k, 256 * k + 256)])
+                 [("tab", 0, NS), ("offs", h0, h0 + 32)], [("sg", 256 * k, 256 * k + 256)])
         for k in range(4):
             score_gather("V" if t == 1 and k == 0 else "S", k)
         if t == 0:
@@ -363,73 +408,86 @@ def rank_program(g, core, T, topo):
         if t == 0:
             p = lambda k: T.pi[:, 16 * k:16 * k + 16]
             pr = lambda k: ("pi", 16 * k, 16 * k + 16)
-            ts(p(0), p(0), 5, A.logical_shift_right, [pr(0)], [pr(0)], 3, A.bitwise_and)
-            ts(p(5), p(1), 4, A.logical_shift_right, [pr(1)], [pr(5)], 1, A.bitwise_and)
-            ts(p(1), p(1), 15, A.bitwise_and, [pr(1)], [pr(1)])
-            ts(p(3), p(0), float(a), A.is_equal, [pr(0)], [pr(3)], -256.0, A.mult)
-            ts(p(4), p(0), 64.0, A.mult, [pr(0)], [pr(4)], 256.0, A.add)
-            tt(p(1), p(1), p(2), A.add, [pr(1), pr(2)], [pr(1)])
-            tt(p(3), p(3), p(4), A.add, [pr(3), pr(4)], [pr(3)])
-            tt(p(3), p(3), p(1), A.add, [pr(3), pr(1)], [pr(3)])
-            copy("V", T.pko[:], p(3), [pr(3)], [("pko", 0, 16)])
             if len(branch) > 1:
+                ts(p(5), p(1), 4, A.logical_shift_right, [pr(1)], [pr(5)], 1, A.bitwise_and)
                 s0, s1 = SLOT[branch[1][0]], SLOT[branch[1][1]]
                 lo = min(s0, s1)
                 ts(T.tau[:, 0:1], T.pi[:, 80:81], float(NS * (s1 - s0)), A.mult, [pr(5)], [("tau", 0, 1)], float(NS * (s0 - lo)), A.add)
-            quant("vq", "vs", 0, 128, "vt", 0)
+            if 3 in slots:
+                fill("tab", 3 * NS, 4 * NS, 0.0)
 
-        n = 0
-        for q in range(4):
-            for b in range(4):
-                mx(n % 4, "bq", "bs", 128 * (4 * q + b), lq, ls, 0, 512)
+        done = [0]
+
+        def window(m):
+            for n in range(done[0], min(16, done[0] + m)):
+                q, b = n // 4, n % 4
+                mx(n % 4, "bq", "bs", 128 * n, lq, ls, 0, 512)
                 lo = NS * b + 512 * q
                 copy("S", T.win[:, lo:lo + 512], T.ps[:, 512 * (n % 4):512 * (n % 4) + 512], [bank(n % 4)], [("win", lo, lo + 512)])
-                n += 1
+            done[0] = min(16, done[0] + m)
 
-        turn = [0]
-
-        def step(offc, lo, hi, row):
-            copy("V", T.rows[:, 256 * row:256 * row + 256], T.tab[:, NS * lo:NS * hi].indirect(T.off[:, offc:offc + 16]),
-                 [("tab", NS * lo, NS * hi), ("off", offc, offc + 16)], [("rows", 256 * row, 256 * row + 256)])
-
-        def turn_row(row):
-            c = 256 * (turn[0] % 2)
-            turn[0] += 1
-            op("V", lambda: V.transpose(T.trs[:, c:c + 256], T.rows[:, 256 * row:256 * row + 256]),
-               [("rows", 256 * row, 256 * row + 256)], [("trs", c, c + 256)])
-            return ("trs", c)
-
-        cur, power, oc = ("rin", 8), 1, 0
-        for tb, make in MAIN[:nmain]:
-            copy("V", T.off[:, oc:oc + 16], T[cur[0]][:, cur[1]:cur[1] // 256 * 256 + 256:16],
-                 [(cur[0], cur[1], cur[1] + 248)], [("off", oc, oc + 16)])
+        steps, power = [], 1
+        for i, (tb, make) in enumerate(MAIN[:nmain]):
             power += tb
-            row = SLOT[power] if make else 0
-            step(oc, SLOT[tb], SLOT[tb] + 1, row)
-            if make:
-                table(row, T.rows[0:128:16, 256 * row:256 * row + 256], [("rows", 256 * row, 256 * row + 256)], "Y")
-            if power < xb or power == xb:
-                cur = turn_row(row)
-            elif tb != MAIN[nmain - 1][0] or not make:
-                cur = turn_row(row)
-            oc = 16 - oc
-        if xb == 1:
-            cur = ("rin", 8)
+            steps.append(("plain", SLOT[tb], SLOT[tb], SLOT[power] if make else 0, make, power <= xb or i < nmain - 1))
         for k, (p0, p1) in enumerate(branch):
-            s0, s1 = SLOT[p0], SLOT[p1]
-            lo, hi = min(s0, s1), max(s0, s1) + 1
-            end = cur[1] // 256 * 256 + 256
-            rd = [(cur[0], cur[1], cur[1] + 248)]
-            if k % 2 == 0:
-                for u, s in ((0, s0), (1, s1)):
-                    c = cur[1] + 16 * (h if k == 0 else u)
-                    ts(T.off[:, oc + u:oc + 16:2], T[cur[0]][:, c:end:32], float(NS * (s - lo)), A.add, rd, [("off", oc + u, oc + u + 1)])
+            steps.append((("first", "group", "column")[k], SLOT[p0], SLOT[p1], 7 + k % 2, 0, True))
+
+        def source(i):
+            if i == 0 or (i == nmain and xb == 1):
+                return "rin", 0, 8
+            return "trs", 256 * ((i - 1) % 2), 0
+
+        def cast(i, u):
+            buf, base, c0 = source(i)
+            lo = base + 128 * u
+            rd = [(buf, lo, lo + 128)]
+            if i == len(steps):
+                copy("V", T.offf[:, 8 * u:8 * u + 8], T[buf][:, lo + c0:lo + 128:16], rd, [("offf", 8 * u, 8 * u + 8)])
+                return
+            kind, s0, s1 = steps[i][:3]
+            oc, first = 16 * (i % 2) + 8 * u, min(s0, s1)
+            if kind == "plain":
+                copy("V", T.off[:, oc:oc + 8], T[buf][:, lo + c0:lo + 128:16], rd, [("off", oc, oc + 8)])
+            elif kind == "group":
+                ts(T.off[:, oc:oc + 8], T[buf][:, lo + c0:lo + 128:16], T.tau[:, 0:1], A.add, rd + [("tau", 0, 1)], [("off", oc, oc + 8)])
             else:
-                ts(T.off[:, oc:oc + 16], T[cur[0]][:, cur[1]:end:16], T.tau[:, 0:1], A.add, rd + [("tau", 0, 1)], [("off", oc, oc + 16)])
-            step(oc, lo, hi, 0 if k % 2 else 7)
-            cur = turn_row(0 if k % 2 else 7)
-            oc = 16 - oc
-        copy("V", T.offf[:], T.trs[:, cur[1]:cur[1] + 256:16], [("trs", cur[1], cur[1] + 256)], [("offf", 0, 16)])
+                for w, s in ((0, s0), (1, s1)):
+                    c = lo + c0 + 16 * (h if kind == "first" else w)
+                    ts(T.off[:, oc + w:oc + 8:2], T[buf][:, c:lo + 128:32], float(NS * (s - first)), A.add, rd, [("off", oc + w, oc + w + 1)])
+
+        def gather(i, u, q):
+            kind, s0, s1, row = steps[i][:4]
+            oc, lo, hi, c = 16 * (i % 2) + 8 * u, NS * min(s0, s1), NS * max(s0, s1) + NS, 256 * row + 128 * u
+            copy(q, T.rows[:, c:c + 128], T.tab[:, lo:hi].indirect(T.off[:, oc:oc + 8]),
+                 [("tab", lo, hi), ("off", oc, oc + 8)], [("rows", c, c + 128)])
+
+        def turn(i, u):
+            if steps[i][5]:
+                c, d = 256 * steps[i][3] + 128 * u, 256 * (i % 2) + 128 * u
+                op("V", lambda: V.transpose(T.trs[:, d:d + 128], T.rows[:, c:c + 128]), [("rows", c, c + 128)], [("trs", d, d + 128)])
+
+        for i in range(len(steps)):
+            cast(i, 0)
+            if i:
+                turn(i - 1, 1)
+                gather(i, 0, "V")
+                cast(i, 1)
+            else:
+                cast(i, 1)
+                gather(i, 0, "V")
+            gather(i, 1, "S") if i < HELPED else None
+            turn(i, 0)
+            gather(i, 1, "V") if i >= HELPED else None
+            row = steps[i][3]
+            if steps[i][4]:
+                table(row, T.rows[0:128:16, 256 * row:256 * row + 256], [("rows", 256 * row, 256 * row + 256)], "YS" if i < HELPED else "Y")
+            if i >= 2:
+                window(1 if i < HELPED - 1 else 16)
+        window(16)
+        cast(len(steps), 0)
+        turn(len(steps) - 1, 1)
+        cast(len(steps), 1)
 
         for b in range(4):
             copy("VS"[b % 2], T[gt][:, b:1024:4], T.win[:, NS * b:NS * b + NS].indirect(T.offf[:]),
@@ -441,7 +499,17 @@ def rank_program(g, core, T, topo):
              lambda d: T[gs][:, 256 + 64 * a:320 + 64 * a], [(gs, 0, 256)])
         arrive("aX%d" % t, [(gq, 256, 512), (gs, 256, 512)])
 
-        if t == 1:
+        if t == 0:
+            ts(p(0), p(0), 5, A.logical_shift_right, [pr(0)], [pr(0)], 3, A.bitwise_and)
+            ts(p(1), p(1), 15, A.bitwise_and, [pr(1)], [pr(1)])
+            ts(p(3), p(0), float(a), A.is_equal, [pr(0)], [pr(3)], -256.0, A.mult)
+            ts(p(4), p(0), 64.0, A.mult, [pr(0)], [pr(4)], 256.0, A.add)
+            tt(p(1), p(1), p(2), A.add, [pr(1), pr(2)], [pr(1)])
+            tt(p(3), p(3), p(4), A.add, [pr(3), pr(4)], [pr(3)])
+            tt(p(3), p(3), p(1), A.add, [pr(3), pr(1)], [pr(3)])
+            copy("V", T.pko[:], p(3), [pr(3)], [("pko", 0, 16)])
+            unit_tiles()
+        else:
             copy("V", T.prow[:], T.tab[:, NS * NAT:NS * NAT + NS].indirect(T.offf[:]),
                  [("tab", NS * NAT, NS * NAT + NS), ("offf", 0, 16)], [("prow", 0, 256)])
             dmas("dpl", [("Y", T.dpo[d % 4], T.prow[0:128:16, 64 * (d % 4):64 * (d % 4) + 64]) for d in served(r)],
@@ -454,6 +522,7 @@ def rank_program(g, core, T, topo):
             outs = [("Y", T.pl[2 * c:2 * c + 2, 64 * ((q - c) % 4):64 * ((q - c) % 4) + 64], T.dpi[c, 32 * q:32 * q + 32, :])
                     for c in range(4) if c != a for q in range(4)]
             dmas("stg", outs, [("dpi", 0, 4)], [])
+            quant("vq", "vs", 0, 128, "vt", 0)
 
         op("V", lambda: V.tensor_copy(T[pq][:].bitcast(dt.uint32), T[gq][:, 0:512].bitcast(dt.uint32).indirect(T.pko[:])),
            [(gq, 0, 512), ("pko", 0, 16)], [(pq, 0, 256)])
@@ -483,7 +552,7 @@ def rank_program(g, core, T, topo):
          + [("S", T.osc[4 * k:4 * k + 4, :], T.xs2[32 * k:32 * k + 4, :]) for k in range(4)],
          [("xq2", 0, 256), ("xs2", 0, 256)], [])
     copy("V", T.yt[:], T.ps[:, 512 * 7:512 * 7 + 256], [bank(7)], [("yt", 0, 256)])
-    dmas("ldx", [("Y", T.y[:], T.yt[:])], [("yt", 0, 256)], [])
+    dmas("ldu", [("S", T.y[:], T.yt[:])], [("yt", 0, 256)], [])
     for s in SEMAPHORES:
         if count[s]:
             wait("G", (s, count[s]))

@@ -3,33 +3,32 @@ from concourse.mybir import dt, AluOpType, ActivationFunctionType
 
 F32, BF, I32, U16, U8, X4 = "float32", "bfloat16", "int32", "uint16", "uint8", "float8_e4m3fn_x4"
 NS = 2048
-NAT = 7
+NAT = 4
 
 SCRATCH = {
     "ps": ("psum", [128, 4096], F32),
-    "tab": ("sbuf", [128, 8 * NS], F32),
+    "tab": ("sbuf", [128, 5 * NS], F32),
     "win": ("sbuf", [128, 4 * NS], BF),
     "ut": ("sbuf", [128, 512], BF), "vt": ("sbuf", [128, 512], BF),
     "uq": ("sbuf", [128, 128], X4), "us": ("sbuf", [128, 128], U8),
     "vq": ("sbuf", [128, 128], X4), "vs": ("sbuf", [128, 128], U8),
     "wq": ("sbuf", [128, 512], X4), "wp": ("sbuf", [128, 512], U8),
-    "cb": ("sbuf", [128, 904], BF), "cb2": ("sbuf", [128, 520], BF),
-    "io1": ("sbuf", [128, 224], F32), "io2": ("sbuf", [128, 128], F32),
-    "rq": ("sbuf", [128, 896], X4), "rs": ("sbuf", [128, 896], U8),
+    "cb": ("sbuf", [128, 520], BF), "cb2": ("sbuf", [128, 520], BF),
+    "io1": ("sbuf", [128, 128], F32), "io2": ("sbuf", [128, 128], F32),
+    "rq": ("sbuf", [128, 512], X4), "rs": ("sbuf", [128, 512], U8),
     "bq": ("sbuf", [128, 2048], X4), "bs": ("sbuf", [128, 2048], U8),
-    "sa": ("sbuf", [128, 24], I32), "sb": ("sbuf", [128, 56], I32),
-    "eb": ("sbuf", [128, 40], I32), "st": ("sbuf", [128, 16], U16),
-    "lc": ("sbuf", [128, 128], U16), "rc": ("sbuf", [128, 128], U16),
-    "offs": ("sbuf", [128, 64], U16), "ei": ("sbuf", [128, 128], I32),
+    "sb": ("sbuf", [128, 32, 16], I32), "sr": ("sbuf", [128, 8, 16], F32), "sd": ("sbuf", [128, 8, 8], F32),
+    "so": ("sbuf", [128, 8, 8], F32), "se": ("sbuf", [128, 8, 8], F32), "sl": ("sbuf", [128, 8, 8], F32),
+    "sa": ("sbuf", [128, 4, 16], F32), "ei": ("sbuf", [128, 256], I32),
+    "offs": ("sbuf", [128, 64], U16),
     "a0": ("sbuf", [128, 64], F32), "a1": ("sbuf", [128, 64], F32), "b0": ("sbuf", [128, 32], F32),
     "mm": ("sbuf", [128, 32], F32), "w1": ("sbuf", [128, 64], F32),
     "sg": ("sbuf", [128, 1024], F32), "tr": ("sbuf", [128, 1024], F32),
-    "rin": ("sbuf", [128, 256], F32), "rows": ("sbuf", [128, 9 * 256], F32), "trs": ("sbuf", [128, 512], F32),
+    "rin": ("sbuf", [128, 256], F32), "rows": ("sbuf", [128, 8 * 256], F32), "trs": ("sbuf", [128, 512], F32),
     "off": ("sbuf", [128, 64], U16), "offf": ("sbuf", [128, 16], U16),
-    "pi": ("sbuf", [128, 96], I32), "pko": ("sbuf", [128, 16], U16),
-    "tau": ("sbuf", [128, 8], F32),
+    "pi": ("sbuf", [128, 16], I32), "tau": ("sbuf", [128, 8], F32),
     "srow": ("sbuf", [128, 256], F32), "prow": ("sbuf", [128, 256], F32), "yt": ("sbuf", [128, 256], F32),
-    "dpo": ("dram", [4, 128, 4], F32), "dpi": ("dram", [4, 128, 4], F32),
+    "dpo": ("dram", [4, 128, 4], F32), "dpi": ("dram", [4, 128, 4], F32), "dsc": ("dram", [8, 128, 8], I32),
 }
 for _t in range(3):
     SCRATCH["x%d" % _t] = ("sbuf", [128, 1024], BF)
@@ -40,33 +39,37 @@ for _t in range(2):
     SCRATCH["tl%d" % _t] = ("sbuf", [128, 1024], BF)
     SCRATCH["tq%d" % _t] = ("sbuf", [128, 256], X4)
     SCRATCH["ts%d" % _t] = ("sbuf", [128, 256], U8)
-    SCRATCH["fq%d" % _t] = ("sbuf", [128, 256], X4)
-    SCRATCH["fs%d" % _t] = ("sbuf", [128, 256], U8)
+    SCRATCH["fq%d" % _t] = ("sbuf", [128, 128], X4)
+    SCRATCH["fs%d" % _t] = ("sbuf", [128, 128], U8)
     SCRATCH["lq%d" % _t] = ("sbuf", [128, 512], X4)
     SCRATCH["ls%d" % _t] = ("sbuf", [128, 512], U8)
     SCRATCH["gt%d" % _t] = ("sbuf", [128, 1024], BF)
-    SCRATCH["gq%d" % _t] = ("sbuf", [128, 512], X4)
-    SCRATCH["gs%d" % _t] = ("sbuf", [128, 512], U8)
-    SCRATCH["pq%d" % _t] = ("sbuf", [128, 256], X4)
-    SCRATCH["pp%d" % _t] = ("sbuf", [128, 256], U8)
+    SCRATCH["gq%d" % _t] = ("sbuf", [128, 256], X4)
+    SCRATCH["gs%d" % _t] = ("sbuf", [128, 256], U8)
+    SCRATCH["zq%d" % _t] = ("sbuf", [128, 512], X4)
+    SCRATCH["zs%d" % _t] = ("sbuf", [128, 512], U8)
     SCRATCH["ht%d" % _t] = ("sbuf", [128, 1024], BF)
     SCRATCH["hq%d" % _t] = ("sbuf", [128, 256], X4)
     SCRATCH["hs%d" % _t] = ("sbuf", [128, 256], U8)
 
 SEMAPHORES = (["cV", "cS", "cP", "cG", "sent", "ldx", "ldu", "lda", "ldb", "ldw", "ldv", "stg", "own", "dpl", "outs",
-               "aC", "aP"] + ["tb%d" % k for k in range(7)]
-              + ["aS0", "aS1", "aT0", "aT1", "aX0", "aX1", "hq0", "hq1", "hs0", "hs1"])
+               "aC", "aP"] + ["tb%d" % k for k in range(4)]
+              + ["aS0", "aS1", "aT0", "aT1", "hq0", "hq1", "hs0", "hs1"]
+              + ["aX%d%d" % (t, c) for t in range(2) for c in range(4)])
 
-MAIN = [(1, 0), (1, 1), (1, 0), (1, 1), (3, 0), (3, 1), (5, 0), (5, 1), (11, 0), (11, 1)]
-PLAN = {0: (0, 1, [(0, 1)]),
-        1: (2, 1, [(1, 1), (1, 3), (1, 3)]),
-        2: (6, 11, [(1, 5), (1, 5), (3, 11)]),
-        3: (10, 43, [(5, 21), (5, 21), (11, 43)])}
-SLOT = {1: 1, 3: 2, 5: 3, 11: 4, 21: 5, 43: 6, 0: 2}
-HELPED = 6
+PLAN = {0: ([], [(0, 1)], {1: 1, 0: 2}),
+        1: ([(1, 0), (1, 1)], [(1, 1), (1, 3), (1, 3)], {1: 1, 3: 0}),
+        2: ([(1, 0), (1, 1), (1, 0), (1, 1), (3, 0), (3, 1)], [(1, 5), (1, 5), (3, 11)], {1: 1, 3: 0, 5: 2, 11: 3}),
+        3: ([(1, 0), (1, 1), (1, 0), (3, 1), (3, 0), (7, 1), (3, 0), (17, 1)], [(3, 17), (7, 37), (17, 37)],
+            {1: 1, 3: 0, 7: 1, 17: 2, 37: 3})}
+EARLY = {"S": [[4, 4, 1, 2, 2, 2, 2, 2, 2, 2, 2, 2, 0], [4, 5, 1, 2, 2, 2, 2, 2, 2, 2, 2, 0, 0]],
+         "V": [[0, 2, 0, 0, 1, 0, 1, 0, 1, 0, 0, 0, 0], [0, 4, 0, 0, 1, 0, 1, 0, 0, 0, 0, 0, 0]]}
+LATE = {"S": [[0, 0, 0, 2, 3, 3, 3, 3, 2, 2, 2, 2, 2], [0, 0, 2, 3, 3, 3, 3, 2, 2, 2, 2, 2, 2]],
+        "V": [[0, 0, 0, 0, 2, 2, 2, 2, 2, 2, 2, 2, 2], [0, 0, 0, 2, 2, 2, 2, 2, 2, 2, 2, 2, 2]]}
+LAND = [0, 192, 256, 448]
 
 
-def masks(topo, src, dsts):
+def masks(topo, src, dsts, cap=16):
     far = [d for d in dsts if topo.chip(d) != topo.chip(src)]
     near = [d for d in dsts if topo.chip(d) == topo.chip(src)]
     out, used = {}, []
@@ -81,7 +84,7 @@ def masks(topo, src, dsts):
         while grown:
             grown = False
             for i in range(len(group)):
-                if n[i] == min(n) and sum(n) + n[i] <= len(eng):
+                if n[i] == min(n) and sum(n) + n[i] <= len(eng) and 2 * n[i] <= cap:
                     n[i] *= 2
                     grown = True
         k = 0
@@ -92,15 +95,16 @@ def masks(topo, src, dsts):
 
 
 def helpers(topo, cores, c):
-    idle = [x for x in topo.cores_of(c) if x not in cores and topo.die(x) == topo.die(c)]
-    one = [x for x in idle if all(topo.may_write(x, d) for d in cores)][0]
-    two = [x for x in idle if x != one][0]
-    easy = [d for d in cores if d != c and topo.may_write(two, d)]
-    return {one: [d for d in cores if d != c and d not in easy], two: easy}
+    def idle(x):
+        return [y for y in topo.cores_of(x) if y not in cores and topo.die(y) == topo.die(c)]
+    mate = [d for d in cores if topo.mates(topo.chip(d), topo.chip(c))][0]
+    here = [d for d in cores if d != c and (topo.chip(d) == topo.chip(c) or topo.same_plane(topo.chip(d), topo.chip(c)))]
+    rest = [d for d in cores if d != c and d not in here]
+    return {x: [d for d in to if cores.index(d) % 4 != 3] for x, to in ((idle(c)[0], here), (idle(mate)[1], rest))}
 
 
-def fused(g, T, topo, src, dsts, sem, src_of, dst_of):
-    m = masks(topo, src, dsts)
+def fused(g, T, topo, src, dsts, sem, src_of, dst_of, cap=16):
+    m = masks(topo, src, dsts, cap)
     tr = []
     for d in dsts:
         rid, pid, _ = topo.addr(d)
@@ -118,7 +122,7 @@ def hand_on(g, core, T, topo):
             continue
         n, sent = len(masks(topo, c, list(hp))[core]), 0
         for t in range(2):
-            lo = lambda d: 64 * (cores.index(d) % 4)
+            lo = lambda d: 64 * (cores.index(d) % 2)
             g.wait_ge(T.sem["hq%d" % t], n)
             sent += fused(g, T, topo, core, hp[core], "aT%d" % t, lambda d: T["fq%d" % t][:, lo(d):lo(d) + 64].bitcast(dt.uint8),
                           lambda d: T["lq%d" % t][:, 64 * s:64 * s + 64].bitcast(dt.uint8))
@@ -166,12 +170,12 @@ def rank_program(g, core, T, topo):
     def op(q, call, reads, writes):
         ex = [x for x in reads if x[0] == "ps"]
         reads = [x for x in reads if x[0] != "ps"]
-        writes = list(writes) + ex
-        need(q, reads, writes)
+        other = [x for x in ex if any(l2 < x[2] and x[1] < h2 and tok[0] != "c" + q for l2, h2, w2, tok in acc.get("ps", []))]
+        need(q, reads, list(writes) + other)
         s = "c" + q
         count[s] += 1
         call().then_inc(T.sem[s], 1)
-        note(reads, writes, (s, count[s]))
+        note(reads, list(writes) + ex, (s, count[s]))
 
     def dmas(sem, items, reads, writes):
         for q in sorted({it[0] for it in items}):
@@ -183,13 +187,13 @@ def rank_program(g, core, T, topo):
             count[sem] += 16
         note(reads, writes, (sem, count[sem]))
 
-    def send(sem, peers, src_of, dst_of, reads):
+    def send(sem, peers, src_of, dst_of, reads, cap=16):
         need("G", reads, [])
-        count["sent"] += fused(g, T, topo, core, [cores[d] for d in peers(r)], sem,
-                               lambda c: src_of(cores.index(c)), lambda c: dst_of(cores.index(c)))
+        count["sent"] += fused(g, T, topo, core, [cores[d] for d in peers(r)], sem(r),
+                               lambda c: src_of(cores.index(c)), lambda c: dst_of(cores.index(c)), cap)
         for s in range(N):
             if r in peers(s):
-                count[sem] += len(masks(topo, cores[s], [cores[d] for d in peers(s)])[core])
+                count[sem(s)] += len(masks(topo, cores[s], [cores[d] for d in peers(s)], cap)[core])
 
     def arrive(sem, writes):
         for b, lo, hi in writes:
@@ -200,6 +204,9 @@ def rank_program(g, core, T, topo):
 
     def served(s):
         return [4 * (s // 4) + (s + k) % 4 for k in range(1, 4)]
+
+    def last(s):
+        return [d for d in everyone(s) if d % 4 == 3]
 
     def bank(k):
         return ("ps", 512 * k, 512 * k + 512)
@@ -240,23 +247,26 @@ def rank_program(g, core, T, topo):
     def codes(name, lo, hi):
         return T[name][:, lo:hi].bitcast(dt.uint8)
 
-    dmas("ldx", [("Y", T.x0[:], T.x[:])], [], [("x0", 0, 1024)])
-    dmas("ldu", [("S", T.ut[:], T.u[:])], [], [("ut", 0, 512)])
-    dmas("lda", [("Y", T.sa[16 * G:16 * G + 16, 0:20], T.sc[:, 32 * (G % 2) + 4 * (G // 2):32 * (G % 2) + 4 * (G // 2) + 20])
-                 for G in range(8)], [], [("sa", 0, 24)])
-    dmas("ldb", [("S", T.sb[16 * G:16 * G + 16, 0:51], T.sc[:, G % 2 + 4 * (G // 2):G % 2 + 4 * (G // 2) + 51])
-                 for G in range(8)], [], [("sb", 0, 56)])
+    def whole(name):
+        return (name, 0, 1 << 20)
 
+    main, branch, slot = PLAN[a]
+    nmain = len(main)
+    pieces = EARLY if a == 3 else LATE
+    hp = helpers(topo, cores, core)
+
+    dmas("lda", [("Y", T.dsc[r], T.sc[:])], [], [("dsc", r, r + 1)])
+    dmas("ldu", [("S", T.ut[:], T.u[:])], [], [("ut", 0, 512)])
+    dmas("ldx", [("Y", T.x0[:], T.x[:])], [], [("x0", 0, 1024)])
+    iota("pi", 0, 16, [[0, 16]], 0, 1, False)
     iota("io2", 0, 128, [[0, 4], [-1, 32]], 0, 1)
     iota("io1", 0, 128, [[-1, 128]], 0, 1)
-    iota("io1", 128, 224, [[-1, 96]], 0, 1)
-    iota("pi", 0, 16, [[-32, 4], [0, 4]], 128, 1, False)
-    iota("pi", 16, 32, [[0, 16]], 0, 1, False)
-    iota("pi", 32, 48, [[0, 4], [16, 4]], 0, 0, False)
-    fill("cb2", 0, 520, 0.0)
-    fill("a0", 0, 64, 0.0)
-    fill("b0", 0, 32, 0.0)
-    fill("rin", 0, 256, 0.0)
+    send(lambda s: "aC", everyone, lambda d: T.dsc[r], lambda d: T.dsc[r], [("dsc", r, r + 1)], 1)
+    arrive("aC", [("dsc", 0, N)])
+    fill("tab", 0, NS, 0.0)
+    for u in range(2):
+        lo = NS + 1024 * u
+        copy("S", T.tab[:, lo:lo + 1024], T.tab[:, 1024 * u:1024 * u + 1024], [("tab", 0, NS)], [("tab", lo, lo + 1024)])
 
     def spread_tiles(q):
         ts(T.cb2[:, 3:515:4], T.io2[:], float(32 * q), A.is_equal, [("io2", 0, 128)], [("cb2", 0, 520)])
@@ -264,133 +274,141 @@ def rank_program(g, core, T, topo):
             quant("bq", "bs", 128 * (4 * q + b), 128, "cb2", 3 - b)
 
     def unit_tiles():
-        fill("cb", 0, 904, 0.0)
-        ts(T.cb[:, 3:899:4], T.io1[:], 0.0, A.is_equal, [("io1", 0, 224)], [("cb", 0, 904)])
+        fill("cb", 0, 520, 0.0)
+        ts(T.cb[:, 3:515:4], T.io1[:], 0.0, A.is_equal, [("io1", 0, 128)], [("cb", 0, 520)])
         for b in range(4):
-            quant("rq", "rs", 224 * b, 224, "cb", 3 - b)
+            quant("rq", "rs", 128 * b, 128, "cb", 3 - b)
 
-    def init_slot(k):
-        for u in range(2):
-            lo = NS * k + 1024 * u
-            copy("S", T.tab[:, lo:lo + 1024], T.x0[:], [("x0", 0, 1024)], [("tab", lo, lo + 1024)])
-
-    def table(k, src_of, reads, queues):
-        dmas("tb%d" % k, [(queues[G % len(queues)], T.tab[16 * G:16 * G + 1, NS * k:NS * k + NS], src_of) for G in range(8)],
+    def table(k, src_of, reads):
+        dmas("tb%d" % k, [("YS"[G % 2], T.tab[16 * G:16 * G + 1, NS * k:NS * k + NS], src_of) for G in range(8)],
              reads, [("tab", NS * k, NS * k + NS)])
 
-    spread_tiles(0)
-    nmain, xb, branch = PLAN[a]
-    slots = [0, 1] + [SLOT[p] for p in (3, 5, 11, 21, 43) if any(p in st for st in branch) or any(p == m[0] for m in MAIN[:nmain])]
-    mine = list(helpers(topo, cores, core))
+    def product_half(t, u, q, s):
+        quant("xq%d" % t, "xs%d" % t, 128 * u, 128, "x%d" % t, 512 * u)
+        mx(4 * u, q, s, 0, "xq%d" % t, "xs%d" % t, 128 * u, 128)
+
+    def score_row(u, q):
+        copy(q, T.srow[0:1, 128 * u:128 * u + 128], T.ps[0:1, 2048 * u:2048 * u + 128], [bank(4 * u)], [("srow", 128 * u, 128 * u + 128)])
+
+    quant("uq", "us", 0, 128, "ut", 0)
+    product_half(0, 0, "uq", "us")
+    product_half(0, 1, "uq", "us")
+    score_row(0, "V")
+    score_row(1, "V")
 
     for t in range(2):
-        X, xq, xs, ds = "x%d" % t, "xq%d" % t, "xs%d" % t, "ds%d" % t
+        X, ds = "x%d" % t, "ds%d" % t
         tl, tq, tsc, lq, ls = "tl%d" % t, "tq%d" % t, "ts%d" % t, "lq%d" % t, "ls%d" % t
-        gt, gq, gs, pq, pp = "gt%d" % t, "gq%d" % t, "gs%d" % t, "pq%d" % t, "pp%d" % t
+        gt, gq, gs, zq, zs = "gt%d" % t, "gq%d" % t, "gs%d" % t, "zq%d" % t, "zs%d" % t
         ht, hq, hs = "ht%d" % t, "hq%d" % t, "hs%d" % t
 
-        if t == 0:
-            quant("uq", "us", 0, 128, "ut", 0)
-        quant(xq, xs, 0, 256, X, 0)
-        mx(7, "uq", "us", 0, xq, xs, 0, 256)
-        copy("V", T.srow[0:1, :], T.ps[0:1, 512 * 7:512 * 7 + 256], [bank(7)], [("srow", 0, 256)])
         dmas("stg", [("Y", T[ds][r], T.srow[0:1, :])], [("srow", 0, 256)], [(ds, r, r + 1)])
-        send("aS%d" % t, everyone, lambda d: T[ds][r], lambda d: T[ds][r], [(ds, r, r + 1)])
+        send(lambda s: "aS%d" % t, everyone, lambda d: T[ds][r], lambda d: T[ds][r], [(ds, r, r + 1)], 1)
         arrive("aS%d" % t, [(ds, 0, N)])
 
-        if t == 0:
-            dmas("ldw", [("Y", codes("wq", 0, 512), T.wc[:]), ("Y", T.wp[:], T.ws[:])], [], [("wq", 0, 512), ("wp", 0, 512)])
-            dmas("ldv", [("Y", T.vt[:], T.v[:])], [], [("vt", 0, 512)])
-            for k in slots:
-                if k <= 2:
-                    init_slot(k)
-            for k1 in range(2):
-                for b0 in range(2):
-                    copy("V", T.st[:, 8 * b0 + 2 * k1:8 * b0 + 2 * k1 + 2], T.sa[:, 16 * k1 + 2 * b0:16 * k1 + 2 * b0 + 2],
-                         [("sa", 0, 24)], [("st", 8 * b0 + 2 * k1, 8 * b0 + 2 * k1 + 2)])
-            for b0 in range(2):
-                copy("V", T.eb[:, 4 * b0:4 * b0 + 4], T.sb[:, 2 * b0:2 * b0 + 49:16], [("sb", 0, 56)], [("eb", 4 * b0, 4 * b0 + 4)])
-            e = lambda k: T.eb[:, 8 * k:8 * k + 8]
-            er = lambda k: ("eb", 8 * k, 8 * k + 8)
-            ts(e(1), e(0), 6, A.logical_shift_right, [er(0)], [er(1)], 3, A.bitwise_and)
-            ts(e(2), e(0), 8, A.logical_shift_right, [er(0)], [er(2)])
-            ts(e(3), e(0), 63, A.bitwise_and, [er(0)], [er(3)])
-            ts(e(1), e(1), 512.0, A.mult, [er(1)], [er(1)])
-            ts(e(2), e(2), 64.0, A.mult, [er(2)], [er(2)])
-            tt(e(3), e(3), e(1), A.add, [er(1), er(3)], [er(3)])
-            tt(e(3), e(3), e(2), A.add, [er(2), er(3)], [er(3)])
-            for b0 in range(2):
-                copy("V", T.st[:, 8 * b0 + 4:8 * b0 + 8], T.eb[:, 24 + 4 * b0:28 + 4 * b0], [er(3)], [("st", 8 * b0 + 4, 8 * b0 + 8)])
-            send("aC", everyone, lambda d: T.st[:], lambda d: T.lc[:, 16 * r:16 * r + 16], [("st", 0, 16)])
-            copy("V", T.lc[:, 16 * r:16 * r + 16], T.st[:], [("st", 0, 16)], [("lc", 16 * r, 16 * r + 16)])
-            arrive("aC", [("lc", 0, 128)])
-
         n = 0
-        for c in range(4):
+        for c in (3, 2, 1, 0):
             for q in range(4):
                 blk = (q - c) % 4
-                eng = "S" if t == 1 and n % 3 == 2 else "V"
+                eng = "S" if n % 3 == 2 and (t or c < 2) else "V"
                 n += 1
                 lo = 256 * c + q
                 copy(eng, T[tl][32 * q:32 * q + 32, 256 * c:256 * c + 256], T[X][32 * c:32 * c + 32, 256 * blk:256 * blk + 256],
                      [(X, 0, 1024)], [(tl, lo, lo + 1)])
-        quant(tq, tsc, 0, 256, tl, 0)
+            if c % 2 == 0:
+                quant(tq, tsc, 64 * c, 128, tl, 256 * c)
+            if c == 2:
+                send(lambda s: "aT%d" % t, last, lambda d: codes(tq, 192, 256), lambda d: codes(lq, 64 * r, 64 * r + 64), [(tq, 128, 256)])
+                send(lambda s: "aT%d" % t, last, lambda d: T[tsc][:, 192:256], lambda d: T[ls][:, 64 * r:64 * r + 64], [(tsc, 128, 256)])
         need("G", [(tq, 0, 256), (tsc, 0, 256)], [])
-        count["sent"] += fused(g, T, topo, core, mine, "hq%d" % t, lambda c: codes(tq, 0, 256), lambda c: codes("fq%d" % t, 0, 256))
-        count["sent"] += fused(g, T, topo, core, mine, "hs%d" % t, lambda c: T[tsc][:], lambda c: T["fs%d" % t][:])
+        pair = lambda c: 128 * (cores.index(hp[c][0]) % 4 // 2)
+        count["sent"] += fused(g, T, topo, core, list(hp), "hq%d" % t, lambda c: codes(tq, pair(c), pair(c) + 128),
+                               lambda c: codes("fq%d" % t, 0, 128))
+        count["sent"] += fused(g, T, topo, core, list(hp), "hs%d" % t, lambda c: T[tsc][:, pair(c):pair(c) + 128],
+                               lambda c: T["fs%d" % t][:])
         for c in cores:
             for hc, to in helpers(topo, cores, c).items():
                 if core in to:
                     count["aT%d" % t] += 2 * len(masks(topo, hc, to)[core])
 
+        if t == 0:
+            dmas("ldb", [("YS"[y], T.sb[16 * y:16 * y + 16, 8 * (s % 4) + 4 * (s // 4):8 * (s % 4) + 4 * (s // 4) + 4, :], T.dsc[s])
+                         for s in range(N) for y in range(2)], [("dsc", 0, N)], [whole("sb")])
+        table(0, T[ds][:], [(ds, 0, N)])
         dmas("own", [("Y", codes(lq, 64 * r, 64 * r + 64), codes(tq, 64 * a, 64 * a + 64)),
                      ("Y", T[ls][:, 64 * r:64 * r + 64], T[tsc][:, 64 * a:64 * a + 64])],
-             [(tq, 0, 256), (tsc, 0, 256)], [(lq, 64 * r, 64 * r + 64), (ls, 64 * r, 64 * r + 64)]) if t == 1 else None
-        table(0, T[ds][:], [(ds, 0, N)], "YS")
-        dmas("own", [("Y", codes(lq, 64 * r, 64 * r + 64), codes(tq, 64 * a, 64 * a + 64)),
-                     ("Y", T[ls][:, 64 * r:64 * r + 64], T[tsc][:, 64 * a:64 * a + 64])],
-             [(tq, 0, 256), (tsc, 0, 256)], [(lq, 64 * r, 64 * r + 64), (ls, 64 * r, 64 * r + 64)]) if t == 0 else None
+             [(tq, 0, 256), (tsc, 0, 256)], [(lq, 64 * r, 64 * r + 64), (ls, 64 * r, 64 * r + 64)])
         arrive("aT%d" % t, [(lq, 0, 512), (ls, 0, 512)])
 
         if t == 0:
-            for k in slots:
-                if k > 3:
-                    iota("tab", NS * k, NS * k + NS, [[0, NS]], 0, 0)
-            if a == 0:
-                iota("tab", NS * SLOT[0], NS * SLOT[0] + NS, [[1, NS]], 0, 0)
-            for q in range(1, 4):
-                spread_tiles(q)
-            rc = "lc"
-            if a:
-                rc = "rc"
-                for q in range(4):
-                    q2 = (q + a) % 4
-                    copy("V", T.rc[32 * q2:32 * q2 + 32, :], T.lc[32 * q:32 * q + 32, :], [("lc", 0, 128)], [("rc", q, q + 1)])
+            dmas("ldw", [("Y", codes("wq", 0, 512), T.wc[:]), ("Y", T.wp[:], T.ws[:])], [], [("wq", 0, 512), ("wp", 0, 512)])
+            for k in sorted(set(slot.values())):
+                if k > 1:
+                    iota("tab", NS * k, NS * k + NS, [[1, NS]], 0, 0)
+            fill("cb2", 0, 520, 0.0)
+            fill("a0", 0, 64, 0.0)
+            fill("b0", 0, 32, 0.0)
+            fill("rin", 0, 256, 0.0)
+            ts(T.pi[:, 8:16], T.pi[:, 0:8], 4, A.logical_shift_right, [("pi", 0, 8)], [("pi", 8, 16)], 1, A.bitwise_and)
+            copy("V", T.tau[:, 1:2], T.pi[:, 8:9], [("pi", 8, 16)], [("tau", 1, 2)])
+            spread_tiles(0)
+            spread_tiles(1)
+            spread_tiles(2)
+            for q in range(4):
+                blk = (q - a) % 4
+                copy("V", T.sr[32 * q:32 * q + 32, :, :], T.sb[0:32, :, 4 * blk:4 * blk + 4], [whole("sb")], [("sr", q, q + 1)])
+            tt(T.sd[:], T.sr[:, :, 8:16], T.sr[:, :, 0:8], A.subtract, [whole("sr")], [whole("sd")])
+            ts(T.sd[:], T.sd[:], T.tau[:, 1:2], A.mult, [whole("sd"), ("tau", 1, 2)], [whole("sd")])
             for k1 in range(2):
-                for hh in range(2):
-                    for u in range(2):
-                        o, i = 32 * k1 + 2 * hh + u, 64 * hh + 2 * k1 + u
-                        copy("V", T.offs[:, o:32 * k1 + 32:4], T[rc][:, i:64 * hh + 64:8], [(rc, 0, 128)], [("offs", o, o + 1)])
+                for cb in range(2):
+                    c = 4 * k1 + 2 * cb
+                    tt(T.so[:, 4 * k1:4 * k1 + 4, 4 * cb:4 * cb + 4], T.sr[:, :, c:c + 2], T.sd[:, :, c:c + 2], A.add,
+                       [whole("sr"), whole("sd")], [("so", c, c + 1)])
+            copy("V", T.offs[:], T.so[:], [whole("so")], [("offs", 0, 64)])
         else:
+            dmas("ldv", [("Y", T.vt[:], T.v[:])], [], [("vt", 0, 512)])
             for q in range(4):
                 lo = NS * NAT + 512 * q
                 iota("tab", lo, lo + 512, [[256, 8], [1, 64]], 64 * ((q - a) % 4), 0)
 
-        def score_gather(q, k):
-            h0 = 32 * (k // 2)
-            copy(q, T.sg[:, 256 * k:256 * k + 256], T.tab[:, 0:NS].indirect(T.offs[:, 16 * k:16 * k + 16]),
-                 [("tab", 0, NS), ("offs", h0, h0 + 32)], [("sg", 256 * k, 256 * k + 256)])
+        made, todo = [0], {"S": [], "V": []}
+
+        def window(q, m):
+            for j in range(m):
+                if not todo[q]:
+                    if made[0] == 16:
+                        return
+                    n = made[0]
+                    made[0] += 1
+                    mx(n % 8, "bq", "bs", 128 * n, lq, ls, 0, 512)
+                    todo[q] = [(n, 0), (n, 1)]
+                n, u = todo[q].pop(0)
+                lo, c = NS * (n % 4) + 512 * (n // 4) + 256 * u, 512 * (n % 8) + 256 * u
+                copy(q, T.win[:, lo:lo + 256], T.ps[:, c:c + 256], [bank(n % 8)], [("win", lo, lo + 256)])
+
         for k in range(4):
-            score_gather("V" if t == 1 and k == 0 else "S", k)
+            copy("V" if t == 1 and k == 0 else "S", T.sg[:, 256 * k:256 * k + 256], T.tab[:, 0:NS].indirect(T.offs[:, 16 * k:16 * k + 16]),
+                 [("tab", 0, NS), ("offs", 0, 64)], [("sg", 256 * k, 256 * k + 256)])
         if t == 0:
-            for k1 in range(2):
-                for hh in range(2):
-                    for x in range(2):
-                        o, i = 32 * k1 + 2 * hh + x, 64 * hh + 4 + 2 * x + k1
-                        ts(T.ei[:, o:32 * k1 + 32:4], T[rc][:, i:64 * hh + 64:8], float(512 * a), A.add, [(rc, 0, 128)], [("ei", o, o + 1)])
-            ts(T.ei[:, 64:128], T.ei[:, 0:64], NS - 1, A.bitwise_and, [("ei", 0, 64)], [("ei", 64, 128)])
-            tt(T.a1[:, 0:64:2], T.ei[:, 96:128], T.ei[:, 64:96], A.subtract, [("ei", 64, 128)], [("a1", 0, 1)])
-            copy("V", T.a1[:, 1:64:2], T.ei[:, 64:96], [("ei", 64, 128)], [("a1", 1, 2)])
+            tt(T.se[:], T.sr[:, :, 1:16:2], T.sr[:, :, 0:16:2], A.subtract, [whole("sr")], [whole("se")])
+            ts(T.se[:], T.se[:], T.tau[:, 1:2], A.mult, [whole("se"), ("tau", 1, 2)], [whole("se")])
+            e = lambda k: T.ei[:, 64 * k:64 * k + 64]
+            er = lambda k: ("ei", 64 * k, 64 * k + 64)
+            tt(e(0), T.se[:], T.sr[:, :, 0:16:2], A.add, [whole("se"), whole("sr")], [er(0)])
+            ts(e(1), e(0), float(64 * a), A.add, [er(0)], [er(1)])
+            ts(e(2), e(0), 8, A.logical_shift_right, [er(0)], [er(2)])
+            ts(e(3), e(0), 63, A.bitwise_and, [er(0)], [er(3)])
+            ts(e(1), e(1), 6, A.logical_shift_right, [er(1)], [er(1)], 3, A.bitwise_and)
+            ts(e(2), e(2), 64.0, A.mult, [er(2)], [er(2)])
+            ts(e(1), e(1), 512.0, A.mult, [er(1)], [er(1)])
+            tt(e(3), e(3), e(2), A.add, [er(2), er(3)], [er(3)])
+            tt(T.sl[:], e(3), e(1), A.add, [er(1), er(3)], [whole("sl")])
+            for cb in range(2):
+                for x in range(2):
+                    c, o = 4 * x + cb, 8 * cb + 2 * x
+                    tt(T.sa[:, :, o:8 * cb + 8:4], T.sl[:, :, c + 2], T.sl[:, :, c], A.subtract, [whole("sl")], [("sa", o, o + 1)])
+                    copy("V", T.sa[:, :, o + 1:8 * cb + 8:4], T.sl[:, :, c], [whole("sl")], [("sa", o + 1, o + 2)])
+            copy("V", T.a1[:], T.sa[:], [whole("sa")], [("a1", 0, 64)])
         for k in range(4):
             op("V", lambda: V.transpose(T.tr[:, 256 * k:256 * k + 256], T.sg[:, 256 * k:256 * k + 256]),
                [("sg", 256 * k, 256 * k + 256)], [("tr", 256 * k, 256 * k + 256)])
@@ -402,44 +420,24 @@ def rank_program(g, core, T, topo):
         tt(T.w1[:, 1:64:4], T.w1[:, 1:64:4], T.w1[:, 3:64:4], A.subtract, [("w1", 0, 64)], [("w1", 0, 64)])
         op("V", lambda: V.tensor_tensor_scan(T.rin[:, 0:256:8], T.b0[:], T.w1[:, 1:64:2], 0.0, A.mult, A.add),
            [("b0", 0, 32), ("w1", 0, 64)], [("rin", 0, 256)])
-        op("V", lambda: V.transpose(T.rows[:, 256:512], T.rin[:]), [("rin", 0, 256)], [("rows", 256, 512)])
-        table(1, T.rows[8:128:16, 256:512], [("rows", 256, 512)], "YS")
+        op("V", lambda: V.transpose(T.rows[:, 512:768], T.rin[:]), [("rin", 0, 256)], [("rows", 512, 768)])
+        window("S", pieces["S"][t][0])
+        table(1, T.rows[8:128:16, 512:768], [("rows", 512, 768)])
 
-        if t == 0:
-            p = lambda k: T.pi[:, 16 * k:16 * k + 16]
-            pr = lambda k: ("pi", 16 * k, 16 * k + 16)
-            if len(branch) > 1:
-                ts(p(5), p(1), 4, A.logical_shift_right, [pr(1)], [pr(5)], 1, A.bitwise_and)
-                s0, s1 = SLOT[branch[1][0]], SLOT[branch[1][1]]
-                lo = min(s0, s1)
-                ts(T.tau[:, 0:1], T.pi[:, 80:81], float(NS * (s1 - s0)), A.mult, [pr(5)], [("tau", 0, 1)], float(NS * (s0 - lo)), A.add)
-            if 3 in slots:
-                fill("tab", 3 * NS, 4 * NS, 0.0)
-
-        done = [0]
-
-        def window(m):
-            for n in range(done[0], min(16, done[0] + m)):
-                q, b = n // 4, n % 4
-                mx(n % 4, "bq", "bs", 128 * n, lq, ls, 0, 512)
-                lo = NS * b + 512 * q
-                copy("S", T.win[:, lo:lo + 512], T.ps[:, 512 * (n % 4):512 * (n % 4) + 512], [bank(n % 4)], [("win", lo, lo + 512)])
-            done[0] = min(16, done[0] + m)
+        if t == 0 and len(branch) > 1:
+            s0, s1 = slot[branch[1][0]], slot[branch[1][1]]
+            ts(T.tau[:, 0:1], T.pi[:, 8:9], float(NS * (s1 - s0)), A.mult, [("pi", 8, 16)], [("tau", 0, 1)],
+               float(NS * (s0 - min(s0, s1))), A.add)
 
         steps, power = [], 1
-        for i, (tb, make) in enumerate(MAIN[:nmain]):
+        for i, (tb, make) in enumerate(main):
             power += tb
-            steps.append(("plain", SLOT[tb], SLOT[tb], SLOT[power] if make else 0, make, power <= xb or i < nmain - 1))
+            steps.append(("plain", slot[tb], slot[tb], 1 + slot[power] if make else 0, make))
         for k, (p0, p1) in enumerate(branch):
-            steps.append((("first", "group", "column")[k], SLOT[p0], SLOT[p1], 7 + k % 2, 0, True))
-
-        def source(i):
-            if i == 0 or (i == nmain and xb == 1):
-                return "rin", 0, 8
-            return "trs", 256 * ((i - 1) % 2), 0
+            steps.append((("first", "group", "column")[k], slot[p0], slot[p1], 6 + k % 2, 0))
 
         def cast(i, u):
-            buf, base, c0 = source(i)
+            buf, base, c0 = ("trs", 256 * ((i - 1) % 2), 0) if i and (i, a) != (nmain, 1) else ("rin", 0, 8)
             lo = base + 128 * u
             rd = [(buf, lo, lo + 128)]
             if i == len(steps):
@@ -463,58 +461,55 @@ def rank_program(g, core, T, topo):
                  [("tab", lo, hi), ("off", oc, oc + 8)], [("rows", c, c + 128)])
 
         def turn(i, u):
-            if steps[i][5]:
-                c, d = 256 * steps[i][3] + 128 * u, 256 * (i % 2) + 128 * u
-                op("V", lambda: V.transpose(T.trs[:, d:d + 128], T.rows[:, c:c + 128]), [("rows", c, c + 128)], [("trs", d, d + 128)])
+            c, d = 256 * steps[i][3] + 128 * u, 256 * (i % 2) + 128 * u
+            op("V", lambda: V.transpose(T.trs[:, d:d + 128], T.rows[:, c:c + 128]), [("rows", c, c + 128)], [("trs", d, d + 128)])
 
-        for i in range(len(steps)):
-            cast(i, 0)
+        for i in range(len(steps) + 1):
             if i:
+                turn(i - 1, 0)
                 turn(i - 1, 1)
-                gather(i, 0, "V")
-                cast(i, 1)
-            else:
-                cast(i, 1)
-                gather(i, 0, "V")
-            gather(i, 1, "S") if i < HELPED else None
-            turn(i, 0)
-            gather(i, 1, "V") if i >= HELPED else None
+            cast(i, 0)
+            cast(i, 1)
+            if i == 0:
+                if t == 0:
+                    spread_tiles(3)
+                window("S", pieces["S"][t][1])
+                window("V", pieces["V"][t][1])
+            if i == len(steps):
+                break
+            gather(i, 0, "S")
+            gather(i, 1, "V")
             row = steps[i][3]
             if steps[i][4]:
-                table(row, T.rows[0:128:16, 256 * row:256 * row + 256], [("rows", 256 * row, 256 * row + 256)], "YS" if i < HELPED else "Y")
-            if i >= 2:
-                window(1 if i < HELPED - 1 else 16)
-        window(16)
-        cast(len(steps), 0)
-        turn(len(steps) - 1, 1)
-        cast(len(steps), 1)
+                table(row - 1, T.rows[0:128:16, 256 * row:256 * row + 256], [("rows", 256 * row, 256 * row + 256)])
+            window("S", pieces["S"][t][i + 2])
+            window("V", pieces["V"][t][i + 2])
+        while made[0] < 16 or todo["S"] or todo["V"]:
+            window("S", 2)
+            window("V", 2)
 
         for b in range(4):
             copy("VS"[b % 2], T[gt][:, b:1024:4], T.win[:, NS * b:NS * b + NS].indirect(T.offf[:]),
                  [("win", NS * b, NS * b + NS), ("offf", 0, 16)], [(gt, b, b + 1)])
         quant(gq, gs, 0, 256, gt, 0)
-        send("aX%d" % t, served, lambda d: codes(gq, 64 * (d % 4), 64 * (d % 4) + 64),
-             lambda d: codes(gq, 256 + 64 * a, 320 + 64 * a), [(gq, 0, 256)])
-        send("aX%d" % t, served, lambda d: T[gs][:, 64 * (d % 4):64 * (d % 4) + 64],
-             lambda d: T[gs][:, 256 + 64 * a:320 + 64 * a], [(gs, 0, 256)])
-        arrive("aX%d" % t, [(gq, 256, 512), (gs, 256, 512)])
+        aX = lambda s: "aX%d%d" % (t, s % 4)
+        send(aX, served, lambda d: codes(gq, 64 * (d % 4), 64 * (d % 4) + 64), lambda d: codes(zq, LAND[a], LAND[a] + 64), [(gq, 0, 256)])
+        send(aX, served, lambda d: T[gs][:, 64 * (d % 4):64 * (d % 4) + 64], lambda d: T[zs][:, LAND[a]:LAND[a] + 64], [(gs, 0, 256)])
+        for c in range(4):
+            if c != a:
+                arrive(aX(c), [(zq, LAND[c], LAND[c] + 64), (zs, LAND[c], LAND[c] + 64)])
 
         if t == 0:
-            ts(p(0), p(0), 5, A.logical_shift_right, [pr(0)], [pr(0)], 3, A.bitwise_and)
-            ts(p(1), p(1), 15, A.bitwise_and, [pr(1)], [pr(1)])
-            ts(p(3), p(0), float(a), A.is_equal, [pr(0)], [pr(3)], -256.0, A.mult)
-            ts(p(4), p(0), 64.0, A.mult, [pr(0)], [pr(4)], 256.0, A.add)
-            tt(p(1), p(1), p(2), A.add, [pr(1), pr(2)], [pr(1)])
-            tt(p(3), p(3), p(4), A.add, [pr(3), pr(4)], [pr(3)])
-            tt(p(3), p(3), p(1), A.add, [pr(3), pr(1)], [pr(3)])
-            copy("V", T.pko[:], p(3), [pr(3)], [("pko", 0, 16)])
             unit_tiles()
+            for z in range(2):
+                for c in (64, 320):
+                    quant("zq%d" % z, "zs%d" % z, c, 128, "x0", 0)
         else:
             copy("V", T.prow[:], T.tab[:, NS * NAT:NS * NAT + NS].indirect(T.offf[:]),
                  [("tab", NS * NAT, NS * NAT + NS), ("offf", 0, 16)], [("prow", 0, 256)])
             dmas("dpl", [("Y", T.dpo[d % 4], T.prow[0:128:16, 64 * (d % 4):64 * (d % 4) + 64]) for d in served(r)],
                  [("prow", 0, 256)], [("dpo", 0, 4)])
-            send("aP", served, lambda d: T.dpo[d % 4], lambda d: T.dpi[a], [("dpo", 0, 4)])
+            send(lambda s: "aP", served, lambda d: T.dpo[d % 4], lambda d: T.dpi[a], [("dpo", 0, 4)], 1)
             arrive("aP", [("dpi", 0, 4)])
             outs = [("Y", T.pl[2 * a:2 * a + 2, 64 * ((q - a) % 4):64 * ((q - a) % 4) + 64],
                      T.prow[32 * q:32 * q + 32:16, 64 * a:64 * a + 64]) for q in range(4)]
@@ -524,35 +519,60 @@ def rank_program(g, core, T, topo):
             dmas("stg", outs, [("dpi", 0, 4)], [])
             quant("vq", "vs", 0, 128, "vt", 0)
 
-        op("V", lambda: V.tensor_copy(T[pq][:].bitcast(dt.uint32), T[gq][:, 0:512].bitcast(dt.uint32).indirect(T.pko[:])),
-           [(gq, 0, 512), ("pko", 0, 16)], [(pq, 0, 256)])
-        copy("S", T[pp][:], T[gs][:, 0:512].indirect(T.pko[:]), [(gs, 0, 512), ("pko", 0, 16)], [(pp, 0, 256)])
-        n = 0
-        for k in range(4):
-            for b in range(4):
-                m0 = min(64 * k, 128)
-                mx(n % 8, "rq", "rs", 224 * b + 32 * k, pq, pp, m0, 128)
-                c = 512 * (n % 8) + 64 * k - m0
-                lo = 256 * k + b
-                copy("VS"[n % 2], T[ht][:, lo:256 * k + 256:4], T.ps[:, c:c + 64], [bank(n % 8)], [(ht, lo, lo + 1)])
-                n += 1
-        quant(hq, hs, 0, 256, ht, 0)
-        Xn = "x%d" % (t + 1)
-        for b in range(4):
-            mx(b, "wq", "wp", 128 * b, hq, hs, 0, 256)
-            o, i = T[Xn][:, b:1024:4], T.ps[:, 512 * b:512 * b + 256]
-            if b % 2 == 0:
-                op("S", lambda: S.activation(o, i, ACT.Relu, scale=0.03125), [bank(b)], [(Xn, b, b + 1)])
-            else:
-                ts(o, i, 0.0, A.max, [bank(b)], [(Xn, b, b + 1)], 0.03125, A.mult)
+        def place(c, off, blks):
+            for blk in blks:
+                for b in range(4):
+                    q, lo, k = (blk + c) % 4, 256 * blk + b, 4 * (c % 2) + b
+                    copy("VS"[b % 2], T[ht][32 * c:32 * c + 32, lo:256 * blk + 256:4],
+                         T.ps[32 * q:32 * q + 32, 512 * k + off:512 * k + off + 64], [bank(k)], [(ht, lo + 4 * c, lo + 4 * c + 1)])
 
-    quant("xq2", "xs2", 0, 256, "x2", 0)
-    mx(7, "vq", "vs", 0, "xq2", "xs2", 0, 256)
-    dmas("outs", [("S", T.oc[:], codes("xq2", 0, 256))]
+        order = [a] + [c for c in range(4) if c != a]
+        for c in order:
+            if c == a:
+                m0 = min(64 * a, 128)
+                src, off = (gq, gs, m0), 64 * a - m0
+            else:
+                src, off = (zq, zs, 128 * c), LAND[c] - 128 * c
+            for b in range(4):
+                mx(4 * (c % 2) + b, "rq", "rs", 128 * b, src[0], src[1], src[2], 128)
+            place(c, off, (0, 1))
+            if c == order[-1]:
+                quant(hq, hs, 0, 128, ht, 0)
+            place(c, off, (2, 3))
+
+        Xn = "x%d" % (t + 1)
+        side = ("vq", "vs") if t else ("uq", "us")
+
+        def layer(u):
+            for b in range(4):
+                mx(4 * u + b, "wq", "wp", 128 * b, hq, hs, 128 * u, 128)
+
+        def relu(u):
+            for b in range(4):
+                lo, k = 512 * u + b, 512 * (4 * u + b)
+                o, i = T[Xn][:, lo:512 * u + 512:4], T.ps[:, k:k + 128]
+                if b % 2 == 0:
+                    op("S", lambda: S.activation(o, i, ACT.Relu, scale=0.03125), [bank(4 * u + b)], [(Xn, lo, lo + 1)])
+                else:
+                    ts(o, i, 0.0, A.max, [bank(4 * u + b)], [(Xn, lo, lo + 1)], 0.03125, A.mult)
+
+        layer(0)
+        quant(hq, hs, 128, 128, ht, 512)
+        layer(1)
+        relu(0)
+        product_half(t + 1, 0, *side)
+        relu(1)
+        product_half(t + 1, 1, *side)
+        if t == 0:
+            score_row(0, "S")
+            score_row(1, "V")
+
+    copy("S", T.yt[:, 0:128], T.ps[:, 0:128], [bank(0)], [("yt", 0, 128)])
+    dmas("outs", [("Y", T.oc[:], codes("xq2", 0, 256))]
          + [("S", T.osc[4 * k:4 * k + 4, :], T.xs2[32 * k:32 * k + 4, :]) for k in range(4)],
          [("xq2", 0, 256), ("xs2", 0, 256)], [])
-    copy("V", T.yt[:], T.ps[:, 512 * 7:512 * 7 + 256], [bank(7)], [("yt", 0, 256)])
-    dmas("ldu", [("S", T.y[:], T.yt[:])], [("yt", 0, 256)], [])
+    copy("V", T.yt[:, 128:256], T.ps[:, 2048:2048 + 128], [bank(4)], [("yt", 128, 256)])
+    dmas("ldu", [("Y", T.y[:], T.yt[:])], [("yt", 0, 256)], [])
     for s in SEMAPHORES:
         if count[s]:
             wait("G", (s, count[s]))

@@ -17,9 +17,7 @@ SCRATCH = {
     "io1": ("sbuf", [128, 128], F32), "io2": ("sbuf", [128, 128], F32),
     "rq": ("sbuf", [128, 512], X4), "rs": ("sbuf", [128, 512], U8),
     "bq": ("sbuf", [128, 2048], X4), "bs": ("sbuf", [128, 2048], U8),
-    "sb": ("sbuf", [128, 32, 16], I32), "sr": ("sbuf", [128, 8, 16], F32), "sd": ("sbuf", [128, 8, 8], F32),
-    "so": ("sbuf", [128, 8, 8], F32), "se": ("sbuf", [128, 8, 8], F32), "sl": ("sbuf", [128, 8, 8], F32),
-    "sa": ("sbuf", [128, 4, 16], F32), "ei": ("sbuf", [128, 256], I32),
+    "sb": ("sbuf", [128, 16, 16], I32), "sr": ("sbuf", [128, 8, 8], F32), "so": ("sbuf", [128, 8, 8], F32),
     "offs": ("sbuf", [128, 64], U16),
     "a0": ("sbuf", [128, 64], F32), "a1": ("sbuf", [128, 64], F32), "b0": ("sbuf", [128, 32], F32),
     "mm": ("sbuf", [128, 32], F32), "w1": ("sbuf", [128, 64], F32),
@@ -62,10 +60,10 @@ PLAN = {0: ([], [(0, 1)], {1: 1, 0: 2}),
         2: ([(1, 0), (1, 1), (1, 0), (1, 1), (3, 0), (3, 1)], [(1, 5), (1, 5), (3, 11)], {1: 1, 3: 0, 5: 2, 11: 3}),
         3: ([(1, 0), (1, 1), (1, 0), (3, 1), (3, 0), (7, 1), (3, 0), (17, 1)], [(3, 17), (7, 37), (17, 37)],
             {1: 1, 3: 0, 7: 1, 17: 2, 37: 3})}
-EARLY = {"S": [[4, 4, 1, 2, 2, 2, 2, 2, 2, 2, 2, 2, 0], [4, 5, 1, 2, 2, 2, 2, 2, 2, 2, 2, 0, 0]],
-         "V": [[0, 2, 0, 0, 1, 0, 1, 0, 1, 0, 0, 0, 0], [0, 4, 0, 0, 1, 0, 1, 0, 0, 0, 0, 0, 0]]}
-LATE = {"S": [[0, 0, 0, 2, 3, 3, 3, 3, 2, 2, 2, 2, 2], [0, 0, 2, 3, 3, 3, 3, 2, 2, 2, 2, 2, 2]],
-        "V": [[0, 0, 0, 0, 2, 2, 2, 2, 2, 2, 2, 2, 2], [0, 0, 0, 2, 2, 2, 2, 2, 2, 2, 2, 2, 2]]}
+EARLY = {"S": [[4, 4, 3, 0, 3, 0, 3, 0, 3, 0, 3, 3, 0], [2, 4, 3, 0, 3, 0, 3, 0, 3, 0, 3, 3, 0]],
+         "V": [[0, 2, 0, 1, 0, 1, 0, 1, 0, 1, 0, 0, 0], [0, 6, 0, 1, 0, 1, 0, 0, 0, 0, 0, 0, 0]]}
+LATE = {"S": [[0, 0, 0, 0, 0, 0, 4, 0, 4, 4, 4, 0, 0], [0, 0, 0, 0, 4, 0, 4, 0, 4, 4, 4, 0, 0]],
+        "V": [[0, 0, 0, 0, 0, 0, 0, 2, 2, 2, 2, 0, 0], [0, 0, 0, 0, 0, 2, 2, 2, 2, 2, 2, 0, 0]]}
 LAND = [0, 192, 256, 448]
 
 
@@ -255,18 +253,21 @@ def rank_program(g, core, T, topo):
     pieces = EARLY if a == 3 else LATE
     hp = helpers(topo, cores, core)
 
-    dmas("lda", [("Y", T.dsc[r], T.sc[:])], [], [("dsc", r, r + 1)])
+    dmas("lda", [("YS"[y], T.dsc[r, 64 * y:64 * y + 64, :], T.sc[:, 32 * y:32 * y + 32]) for y in range(2)], [], [("dsc", r, r + 1)])
     dmas("ldu", [("S", T.ut[:], T.u[:])], [], [("ut", 0, 512)])
     dmas("ldx", [("Y", T.x0[:], T.x[:])], [], [("x0", 0, 1024)])
-    iota("pi", 0, 16, [[0, 16]], 0, 1, False)
     iota("io2", 0, 128, [[0, 4], [-1, 32]], 0, 1)
-    iota("io1", 0, 128, [[-1, 128]], 0, 1)
+    iota("tab", 0, 64 * (4 - a), [[512, 4 - a], [1, 64]], 512 * a, 0)
+    if a:
+        iota("tab", 64 * (4 - a), 256, [[512, a], [1, 64]], 0, 0)
+    iota("pi", 0, 16, [[0, 16]], 0, 1, False)
     send(lambda s: "aC", everyone, lambda d: T.dsc[r], lambda d: T.dsc[r], [("dsc", r, r + 1)], 1)
     arrive("aC", [("dsc", 0, N)])
-    fill("tab", 0, NS, 0.0)
+    for n in (256, 512, 1024):
+        op("S", lambda: S.activation(T.tab[:, n:2 * n], T.tab[:, 0:n], ACT.Identity, bias=float(n // 4)), [("tab", 0, n)], [("tab", n, 2 * n)])
     for u in range(2):
         lo = NS + 1024 * u
-        copy("S", T.tab[:, lo:lo + 1024], T.tab[:, 1024 * u:1024 * u + 1024], [("tab", 0, NS)], [("tab", lo, lo + 1024)])
+        copy("S", T.tab[:, lo:lo + 1024], T.tab[:, 0:1024], [("tab", 0, 1024)], [("tab", lo, lo + 1024)])
 
     def spread_tiles(q):
         ts(T.cb2[:, 3:515:4], T.io2[:], float(32 * q), A.is_equal, [("io2", 0, 128)], [("cb2", 0, 520)])
@@ -290,6 +291,11 @@ def rank_program(g, core, T, topo):
     def score_row(u, q):
         copy(q, T.srow[0:1, 128 * u:128 * u + 128], T.ps[0:1, 2048 * u:2048 * u + 128], [bank(4 * u)], [("srow", 128 * u, 128 * u + 128)])
 
+    fill("cb2", 0, 520, 0.0)
+    fill("a0", 0, 64, 0.0)
+    fill("b0", 0, 32, 0.0)
+    fill("rin", 0, 256, 0.0)
+    spread_tiles(0)
     quant("uq", "us", 0, 128, "ut", 0)
     product_half(0, 0, "uq", "us")
     product_half(0, 1, "uq", "us")
@@ -310,7 +316,7 @@ def rank_program(g, core, T, topo):
         for c in (3, 2, 1, 0):
             for q in range(4):
                 blk = (q - c) % 4
-                eng = "S" if n % 3 == 2 and (t or c < 2) else "V"
+                eng = "S" if n % 3 == 2 and t else "V"
                 n += 1
                 lo = 256 * c + q
                 copy(eng, T[tl][32 * q:32 * q + 32, 256 * c:256 * c + 256], T[X][32 * c:32 * c + 32, 256 * blk:256 * blk + 256],
@@ -332,8 +338,8 @@ def rank_program(g, core, T, topo):
                     count["aT%d" % t] += 2 * len(masks(topo, hc, to)[core])
 
         if t == 0:
-            dmas("ldb", [("YS"[y], T.sb[16 * y:16 * y + 16, 8 * (s % 4) + 4 * (s // 4):8 * (s % 4) + 4 * (s // 4) + 4, :], T.dsc[s])
-                         for s in range(N) for y in range(2)], [("dsc", 0, N)], [whole("sb")])
+            dmas("ldb", [("YS"[s % 2], T.sb[0:32, 4 * (s % 4) + 2 * (s // 4):4 * (s % 4) + 2 * (s // 4) + 2, :], T.dsc[s])
+                         for s in range(N)], [("dsc", 0, N)], [whole("sb")])
         table(0, T[ds][:], [(ds, 0, N)])
         dmas("own", [("Y", codes(lq, 64 * r, 64 * r + 64), codes(tq, 64 * a, 64 * a + 64)),
                      ("Y", T[ls][:, 64 * r:64 * r + 64], T[tsc][:, 64 * a:64 * a + 64])],
@@ -342,28 +348,24 @@ def rank_program(g, core, T, topo):
 
         if t == 0:
             dmas("ldw", [("Y", codes("wq", 0, 512), T.wc[:]), ("Y", T.wp[:], T.ws[:])], [], [("wq", 0, 512), ("wp", 0, 512)])
+            iota("io1", 0, 128, [[-1, 128]], 0, 1)
             for k in sorted(set(slot.values())):
                 if k > 1:
                     iota("tab", NS * k, NS * k + NS, [[1, NS]], 0, 0)
-            fill("cb2", 0, 520, 0.0)
-            fill("a0", 0, 64, 0.0)
-            fill("b0", 0, 32, 0.0)
-            fill("rin", 0, 256, 0.0)
             ts(T.pi[:, 8:16], T.pi[:, 0:8], 4, A.logical_shift_right, [("pi", 0, 8)], [("pi", 8, 16)], 1, A.bitwise_and)
-            copy("V", T.tau[:, 1:2], T.pi[:, 8:9], [("pi", 8, 16)], [("tau", 1, 2)])
-            spread_tiles(0)
             spread_tiles(1)
             spread_tiles(2)
+            if len(branch) > 1:
+                s0, s1 = slot[branch[1][0]], slot[branch[1][1]]
+                ts(T.tau[:, 0:1], T.pi[:, 8:9], float(NS * (s1 - s0)), A.mult, [("pi", 8, 16)], [("tau", 0, 1)],
+                   float(NS * (s0 - min(s0, s1))), A.add)
             for q in range(4):
                 blk = (q - a) % 4
                 copy("V", T.sr[32 * q:32 * q + 32, :, :], T.sb[0:32, :, 4 * blk:4 * blk + 4], [whole("sb")], [("sr", q, q + 1)])
-            tt(T.sd[:], T.sr[:, :, 8:16], T.sr[:, :, 0:8], A.subtract, [whole("sr")], [whole("sd")])
-            ts(T.sd[:], T.sd[:], T.tau[:, 1:2], A.mult, [whole("sd"), ("tau", 1, 2)], [whole("sd")])
             for k1 in range(2):
                 for cb in range(2):
                     c = 4 * k1 + 2 * cb
-                    tt(T.so[:, 4 * k1:4 * k1 + 4, 4 * cb:4 * cb + 4], T.sr[:, :, c:c + 2], T.sd[:, :, c:c + 2], A.add,
-                       [whole("sr"), whole("sd")], [("so", c, c + 1)])
+                    copy("V", T.so[:, 4 * k1:4 * k1 + 4, 4 * cb:4 * cb + 4], T.sr[:, :, c:c + 2], [whole("sr")], [("so", c, c + 1)])
             copy("V", T.offs[:], T.so[:], [whole("so")], [("offs", 0, 64)])
         else:
             dmas("ldv", [("Y", T.vt[:], T.v[:])], [], [("vt", 0, 512)])
@@ -387,31 +389,14 @@ def rank_program(g, core, T, topo):
                 copy(q, T.win[:, lo:lo + 256], T.ps[:, c:c + 256], [bank(n % 8)], [("win", lo, lo + 256)])
 
         for k in range(4):
-            copy("V" if t == 1 and k == 0 else "S", T.sg[:, 256 * k:256 * k + 256], T.tab[:, 0:NS].indirect(T.offs[:, 16 * k:16 * k + 16]),
+            copy("S" if k else "V", T.sg[:, 256 * k:256 * k + 256], T.tab[:, 0:NS].indirect(T.offs[:, 16 * k:16 * k + 16]),
                  [("tab", 0, NS), ("offs", 0, 64)], [("sg", 256 * k, 256 * k + 256)])
-        if t == 0:
-            tt(T.se[:], T.sr[:, :, 1:16:2], T.sr[:, :, 0:16:2], A.subtract, [whole("sr")], [whole("se")])
-            ts(T.se[:], T.se[:], T.tau[:, 1:2], A.mult, [whole("se"), ("tau", 1, 2)], [whole("se")])
-            e = lambda k: T.ei[:, 64 * k:64 * k + 64]
-            er = lambda k: ("ei", 64 * k, 64 * k + 64)
-            tt(e(0), T.se[:], T.sr[:, :, 0:16:2], A.add, [whole("se"), whole("sr")], [er(0)])
-            ts(e(1), e(0), float(64 * a), A.add, [er(0)], [er(1)])
-            ts(e(2), e(0), 8, A.logical_shift_right, [er(0)], [er(2)])
-            ts(e(3), e(0), 63, A.bitwise_and, [er(0)], [er(3)])
-            ts(e(1), e(1), 6, A.logical_shift_right, [er(1)], [er(1)], 3, A.bitwise_and)
-            ts(e(2), e(2), 64.0, A.mult, [er(2)], [er(2)])
-            ts(e(1), e(1), 512.0, A.mult, [er(1)], [er(1)])
-            tt(e(3), e(3), e(2), A.add, [er(2), er(3)], [er(3)])
-            tt(T.sl[:], e(3), e(1), A.add, [er(1), er(3)], [whole("sl")])
-            for cb in range(2):
-                for x in range(2):
-                    c, o = 4 * x + cb, 8 * cb + 2 * x
-                    tt(T.sa[:, :, o:8 * cb + 8:4], T.sl[:, :, c + 2], T.sl[:, :, c], A.subtract, [whole("sl")], [("sa", o, o + 1)])
-                    copy("V", T.sa[:, :, o + 1:8 * cb + 8:4], T.sl[:, :, c], [whole("sl")], [("sa", o + 1, o + 2)])
-            copy("V", T.a1[:], T.sa[:], [whole("sa")], [("a1", 0, 64)])
         for k in range(4):
             op("V", lambda: V.transpose(T.tr[:, 256 * k:256 * k + 256], T.sg[:, 256 * k:256 * k + 256]),
                [("sg", 256 * k, 256 * k + 256)], [("tr", 256 * k, 256 * k + 256)])
+        if t == 0:
+            tt(T.a1[:, 0:64:2], T.tr[:, 513:1024:16], T.tr[:, 1:512:16], A.subtract, [("tr", 0, 1024)], [("a1", 0, 1)])
+            copy("V", T.a1[:, 1:64:2], T.tr[:, 1:512:16], [("tr", 0, 1024)], [("a1", 1, 2)])
         tt(T.a0[:, 1:64:2], T.tr[:, 512:1024:16], T.tr[:, 0:512:16], A.is_gt, [("tr", 0, 1024)], [("a0", 0, 64)])
         tt(T.mm[:], T.tr[:, 512:1024:16], T.tr[:, 0:512:16], A.max, [("tr", 0, 1024)], [("mm", 0, 32)])
         op("V", lambda: V.tensor_tensor_scan(T.w1[:], T.a0[:], T.a1[:], 0.0, A.mult, A.add),
@@ -423,11 +408,6 @@ def rank_program(g, core, T, topo):
         op("V", lambda: V.transpose(T.rows[:, 512:768], T.rin[:]), [("rin", 0, 256)], [("rows", 512, 768)])
         window("S", pieces["S"][t][0])
         table(1, T.rows[8:128:16, 512:768], [("rows", 512, 768)])
-
-        if t == 0 and len(branch) > 1:
-            s0, s1 = slot[branch[1][0]], slot[branch[1][1]]
-            ts(T.tau[:, 0:1], T.pi[:, 8:9], float(NS * (s1 - s0)), A.mult, [("pi", 8, 16)], [("tau", 0, 1)],
-               float(NS * (s0 - min(s0, s1))), A.add)
 
         steps, power = [], 1
         for i, (tb, make) in enumerate(main):
@@ -470,13 +450,13 @@ def rank_program(g, core, T, topo):
                 turn(i - 1, 1)
             cast(i, 0)
             cast(i, 1)
+            if i == len(steps):
+                break
             if i == 0:
                 if t == 0:
                     spread_tiles(3)
                 window("S", pieces["S"][t][1])
                 window("V", pieces["V"][t][1])
-            if i == len(steps):
-                break
             gather(i, 0, "S")
             gather(i, 1, "V")
             row = steps[i][3]

@@ -33,7 +33,7 @@ for _t in range(3):
     SCRATCH["xq%d" % _t] = ("sbuf", [128, 256], X4)
     SCRATCH["xs%d" % _t] = ("sbuf", [128, 256], U8)
 for _t in range(2):
-    SCRATCH["ds%d" % _t] = ("dram", [8, 128, 2], F32)
+    SCRATCH["ds%d" % _t] = ("dram", [8 + 8 * _t, 128, 2], F32)
     SCRATCH["tl%d" % _t] = ("sbuf", [128, 1024], BF)
     SCRATCH["tq%d" % _t] = ("sbuf", [128, 256], X4)
     SCRATCH["ts%d" % _t] = ("sbuf", [128, 256], U8)
@@ -50,20 +50,19 @@ for _t in range(2):
     SCRATCH["hq%d" % _t] = ("sbuf", [128, 256], X4)
     SCRATCH["hs%d" % _t] = ("sbuf", [128, 256], U8)
 
-SEMAPHORES = (["cV", "cS", "cP", "cG", "sent", "ldx", "ldu", "lda", "ldb", "ldw", "ldv", "stg", "own", "dpl", "outs",
-               "aC", "aP"] + ["tb%d" % k for k in range(4)]
+SEMAPHORES = (["cV", "cS", "cP", "cG", "sent", "ldx", "ldu", "lda", "ldb", "ldw", "ldv", "stg", "own", "dpl", "outs", "aC"]
+              + ["tb%d" % k for k in range(4)] + ["aP%d" % k for k in range(4)] + ["pl%d" % k for k in range(4)]
               + ["aS0", "aS1", "aT0", "aT1", "hq0", "hq1", "hs0", "hs1"]
               + ["aX%d%d" % (t, c) for t in range(2) for c in range(4)])
 
-PLAN = {0: ([], [(0, 1)], {1: 1, 0: 2}),
-        1: ([(1, 0), (1, 1)], [(1, 1), (1, 3), (1, 3)], {1: 1, 3: 0}),
-        2: ([(1, 0), (1, 1), (1, 0), (1, 1), (3, 0), (3, 1)], [(1, 5), (1, 5), (3, 11)], {1: 1, 3: 0, 5: 2, 11: 3}),
+PLAN = {0: ([], [(0, 1)], {1: 0, 0: 1}),
+        1: ([(1, 0), (1, 1)], [(1, 1), (1, 3), (1, 3)], {1: 0, 3: 1}),
+        2: ([(1, 0), (1, 1), (1, 0), (1, 1), (3, 0), (3, 1)], [(1, 5), (1, 5), (3, 11)], {1: 0, 3: 1, 5: 2, 11: 3}),
         3: ([(1, 0), (1, 1), (1, 0), (3, 1), (3, 0), (7, 1), (3, 0), (17, 1)], [(3, 17), (7, 37), (17, 37)],
-            {1: 1, 3: 0, 7: 1, 17: 2, 37: 3})}
-EARLY = {"S": [[4, 4, 3, 0, 3, 0, 3, 0, 3, 0, 3, 3, 0], [2, 4, 3, 0, 3, 0, 3, 0, 3, 0, 3, 3, 0]],
-         "V": [[0, 2, 0, 1, 0, 1, 0, 1, 0, 1, 0, 0, 0], [0, 6, 0, 1, 0, 1, 0, 0, 0, 0, 0, 0, 0]]}
-LATE = {"S": [[0, 0, 0, 0, 0, 0, 4, 0, 4, 4, 4, 0, 0], [0, 0, 0, 0, 4, 0, 4, 0, 4, 4, 4, 0, 0]],
-        "V": [[0, 0, 0, 0, 0, 0, 0, 2, 2, 2, 2, 0, 0], [0, 0, 0, 0, 0, 2, 2, 2, 2, 2, 2, 0, 0]]}
+            {1: 0, 3: 1, 7: 0, 17: 2, 37: 3})}
+PIECES = [[6, 4, 3, 0, 3, 0, 3, 0, 3, 0, 3, 3, 0], [6, 4, 3, 0, 3, 0, 3, 0, 3, 0, 2, 2, 0]]
+BEFORE = [4, 6]
+SHARE = [(8, 12, 16), (8, 12, 15)]
 LAND = [0, 192, 256, 448]
 
 
@@ -75,6 +74,8 @@ def masks(topo, src, dsts, cap=16):
         if not group:
             continue
         eng = [e for e in topo.engines(src, group[0]) if e not in used]
+        if group is near:
+            eng.reverse()
         if group is far:
             used = list(eng)
         n = [1] * len(group)
@@ -106,8 +107,9 @@ def fused(g, T, topo, src, dsts, sem, src_of, dst_of, cap=16):
     tr = []
     for d in dsts:
         rid, pid, _ = topo.addr(d)
-        tr.append(RemoteDMATransfer(dst_ids=[DstId(rid=rid, pnc=pid)], dma_engine_mask=sum(1 << e for e in m[d]),
-                                    remote_sem=T.sem[sem], src=src_of(d), dst=dst_of(d)))
+        to = dst_of(d) if isinstance(dst_of(d), list) else [dst_of(d)]
+        tr.append(RemoteDMATransfer(dst_ids=[DstId(rid=rid, pnc=pid)] * len(to), dma_engine_mask=sum(1 << e for e in m[d]),
+                                    remote_sem=T.sem[sem], srcs=[src_of(d)], dsts=to))
     g.remote_dma_fused(tr, local_sem=T.sem.sent)
     return sum(len(m[d]) for d in dsts)
 
@@ -119,8 +121,8 @@ def hand_on(g, core, T, topo):
         if core not in hp:
             continue
         n, sent = len(masks(topo, c, list(hp))[core]), 0
+        lo = lambda d: 64 * (cores.index(d) % 2)
         for t in range(2):
-            lo = lambda d: 64 * (cores.index(d) % 2)
             g.wait_ge(T.sem["hq%d" % t], n)
             sent += fused(g, T, topo, core, hp[core], "aT%d" % t, lambda d: T["fq%d" % t][:, lo(d):lo(d) + 64].bitcast(dt.uint8),
                           lambda d: T["lq%d" % t][:, 64 * s:64 * s + 64].bitcast(dt.uint8))
@@ -206,6 +208,9 @@ def rank_program(g, core, T, topo):
     def last(s):
         return [d for d in everyone(s) if d % 4 == 3]
 
+    def beside(s, d):
+        return topo.chip(cores[s]) == topo.chip(cores[d])
+
     def bank(k):
         return ("ps", 512 * k, 512 * k + 512)
 
@@ -250,8 +255,9 @@ def rank_program(g, core, T, topo):
 
     main, branch, slot = PLAN[a]
     nmain = len(main)
-    pieces = EARLY if a == 3 else LATE
+    late = a == 3
     hp = helpers(topo, cores, core)
+    away = [d % 4 // 2 for d in served(r) if not beside(r, d)][0]
 
     dmas("lda", [("YS"[y], T.dsc[r, 64 * y:64 * y + 64, :], T.sc[:, 32 * y:32 * y + 32]) for y in range(2)], [], [("dsc", r, r + 1)])
     dmas("ldu", [("S", T.ut[:], T.u[:])], [], [("ut", 0, 512)])
@@ -265,23 +271,26 @@ def rank_program(g, core, T, topo):
     arrive("aC", [("dsc", 0, N)])
     for n in (256, 512, 1024):
         op("S", lambda: S.activation(T.tab[:, n:2 * n], T.tab[:, 0:n], ACT.Identity, bias=float(n // 4)), [("tab", 0, n)], [("tab", n, 2 * n)])
-    for u in range(2):
-        lo = NS + 1024 * u
-        copy("S", T.tab[:, lo:lo + 1024], T.tab[:, 0:1024], [("tab", 0, 1024)], [("tab", lo, lo + 1024)])
+
+    later = []
+
+    def spare(n=1):
+        for k in range(min(n, len(later))):
+            later.pop(0)()
 
     def spread_tiles(q):
-        ts(T.cb2[:, 3:515:4], T.io2[:], float(32 * q), A.is_equal, [("io2", 0, 128)], [("cb2", 0, 520)])
+        later.append(lambda: ts(T.cb2[:, 3:515:4], T.io2[:], float(32 * q), A.is_equal, [("io2", 0, 128)], [("cb2", 0, 520)]))
         for b in range(4):
-            quant("bq", "bs", 128 * (4 * q + b), 128, "cb2", 3 - b)
+            later.append(lambda b=b: quant("bq", "bs", 128 * (4 * q + b), 128, "cb2", 3 - b))
 
     def unit_tiles():
-        fill("cb", 0, 520, 0.0)
-        ts(T.cb[:, 3:515:4], T.io1[:], 0.0, A.is_equal, [("io1", 0, 128)], [("cb", 0, 520)])
+        later.append(lambda: fill("cb", 0, 520, 0.0))
+        later.append(lambda: ts(T.cb[:, 3:515:4], T.io1[:], 0.0, A.is_equal, [("io1", 0, 128)], [("cb", 0, 520)]))
         for b in range(4):
-            quant("rq", "rs", 128 * b, 128, "cb", 3 - b)
+            later.append(lambda b=b: quant("rq", "rs", 128 * b, 128, "cb", 3 - b))
 
-    def table(k, src_of, reads):
-        dmas("tb%d" % k, [("YS"[G % 2], T.tab[16 * G:16 * G + 1, NS * k:NS * k + NS], src_of) for G in range(8)],
+    def table(k, src_of, reads, queues="YS"):
+        dmas("tb%d" % k, [(queues[G % len(queues)], T.tab[16 * G:16 * G + 1, NS * k:NS * k + NS], src_of) for G in range(8)],
              reads, [("tab", NS * k, NS * k + NS)])
 
     def product_half(t, u, q, s):
@@ -296,6 +305,7 @@ def rank_program(g, core, T, topo):
     fill("b0", 0, 32, 0.0)
     fill("rin", 0, 256, 0.0)
     spread_tiles(0)
+    spare(5)
     quant("uq", "us", 0, 128, "ut", 0)
     product_half(0, 0, "uq", "us")
     product_half(0, 1, "uq", "us")
@@ -309,14 +319,17 @@ def rank_program(g, core, T, topo):
         ht, hq, hs = "ht%d" % t, "hq%d" % t, "hs%d" % t
 
         dmas("stg", [("Y", T[ds][r], T.srow[0:1, :])], [("srow", 0, 256)], [(ds, r, r + 1)])
-        send(lambda s: "aS%d" % t, everyone, lambda d: T[ds][r], lambda d: T[ds][r], [(ds, r, r + 1)], 1)
-        arrive("aS%d" % t, [(ds, 0, N)])
+        if t:
+            dmas("dpl", [("Y", T[ds][N + r], T.srow[0:1, :])], [("srow", 0, 256)], [(ds, N + r, N + r + 1)])
+        send(lambda s: "aS%d" % t, everyone, lambda d: T[ds][r], lambda d: [T[ds][N * k + r] for k in range(1 + t)], [(ds, r, r + 1)], 1)
+        count["aS%d" % t] *= 1 + t
+        arrive("aS%d" % t, [(ds, 0, 2 * N)])
 
         n = 0
         for c in (3, 2, 1, 0):
             for q in range(4):
                 blk = (q - c) % 4
-                eng = "S" if n % 3 == 2 and t else "V"
+                eng = "S" if n % 3 == 2 else "V"
                 n += 1
                 lo = 256 * c + q
                 copy(eng, T[tl][32 * q:32 * q + 32, 256 * c:256 * c + 256], T[X][32 * c:32 * c + 32, 256 * blk:256 * blk + 256],
@@ -340,7 +353,9 @@ def rank_program(g, core, T, topo):
         if t == 0:
             dmas("ldb", [("YS"[s % 2], T.sb[0:32, 4 * (s % 4) + 2 * (s // 4):4 * (s % 4) + 2 * (s // 4) + 2, :], T.dsc[s])
                          for s in range(N)], [("dsc", 0, N)], [whole("sb")])
-        table(0, T[ds][:], [(ds, 0, N)])
+            table(0, T[ds][:], [(ds, 0, N)])
+        else:
+            dmas("tb0", [("YS"[q % 2], T.tab[32 * q:32 * q + 32:16, 0:NS], T[ds][:]) for q in range(4)], [(ds, 0, 2 * N)], [("tab", 0, NS)])
         dmas("own", [("Y", codes(lq, 64 * r, 64 * r + 64), codes(tq, 64 * a, 64 * a + 64)),
                      ("Y", T[ls][:, 64 * r:64 * r + 64], T[tsc][:, 64 * a:64 * a + 64])],
              [(tq, 0, 256), (tsc, 0, 256)], [(lq, 64 * r, 64 * r + 64), (ls, 64 * r, 64 * r + 64)])
@@ -348,13 +363,14 @@ def rank_program(g, core, T, topo):
 
         if t == 0:
             dmas("ldw", [("Y", codes("wq", 0, 512), T.wc[:]), ("Y", T.wp[:], T.ws[:])], [], [("wq", 0, 512), ("wp", 0, 512)])
-            iota("io1", 0, 128, [[-1, 128]], 0, 1)
-            for k in sorted(set(slot.values())):
-                if k > 1:
-                    iota("tab", NS * k, NS * k + NS, [[1, NS]], 0, 0)
+            for k in sorted(set(slot.values()) - {0}):
+                iota("tab", NS * k, NS * k + NS, [[1, NS]], 0, 0)
+                if k == 1:
+                    iota("io1", 0, 128, [[-1, 128]], 0, 1)
             ts(T.pi[:, 8:16], T.pi[:, 0:8], 4, A.logical_shift_right, [("pi", 0, 8)], [("pi", 8, 16)], 1, A.bitwise_and)
             spread_tiles(1)
             spread_tiles(2)
+            spare(6)
             if len(branch) > 1:
                 s0, s1 = slot[branch[1][0]], slot[branch[1][1]]
                 ts(T.tau[:, 0:1], T.pi[:, 8:9], float(NS * (s1 - s0)), A.mult, [("pi", 8, 16)], [("tau", 0, 1)],
@@ -375,7 +391,7 @@ def rank_program(g, core, T, topo):
 
         made, todo = [0], {"S": [], "V": []}
 
-        def window(q, m):
+        def window(q, m, w=256):
             for j in range(m):
                 if not todo[q]:
                     if made[0] == 16:
@@ -383,14 +399,14 @@ def rank_program(g, core, T, topo):
                     n = made[0]
                     made[0] += 1
                     mx(n % 8, "bq", "bs", 128 * n, lq, ls, 0, 512)
-                    todo[q] = [(n, 0), (n, 1)]
-                n, u = todo[q].pop(0)
-                lo, c = NS * (n % 4) + 512 * (n // 4) + 256 * u, 512 * (n % 8) + 256 * u
-                copy(q, T.win[:, lo:lo + 256], T.ps[:, c:c + 256], [bank(n % 8)], [("win", lo, lo + 256)])
+                    todo[q] = [(n, c) for c in range(0, 512, w)]
+                n, c = todo[q].pop(0)
+                lo, k = NS * (n % 4) + 512 * (n // 4) + c, 512 * (n % 8) + c
+                copy(q, T.win[:, lo:lo + w], T.ps[:, k:k + w], [bank(n % 8)], [("win", lo, lo + w)])
 
-        for k in range(4):
-            copy("S" if k else "V", T.sg[:, 256 * k:256 * k + 256], T.tab[:, 0:NS].indirect(T.offs[:, 16 * k:16 * k + 16]),
-                 [("tab", 0, NS), ("offs", 0, 64)], [("sg", 256 * k, 256 * k + 256)])
+        for q, lo, hi in (("V", 0, 16), ("S", 16, 32), ("S", 32, 48), ("V", 56, 64), ("S", 48, 56)):
+            copy(q, T.sg[:, 16 * lo:16 * hi], T.tab[:, 0:NS].indirect(T.offs[:, lo:hi]),
+                 [("tab", 0, NS), ("offs", 0, 64)], [("sg", 16 * lo, 16 * hi)])
         for k in range(4):
             op("V", lambda: V.transpose(T.tr[:, 256 * k:256 * k + 256], T.sg[:, 256 * k:256 * k + 256]),
                [("sg", 256 * k, 256 * k + 256)], [("tr", 256 * k, 256 * k + 256)])
@@ -399,15 +415,20 @@ def rank_program(g, core, T, topo):
             copy("V", T.a1[:, 1:64:2], T.tr[:, 1:512:16], [("tr", 0, 1024)], [("a1", 1, 2)])
         tt(T.a0[:, 1:64:2], T.tr[:, 512:1024:16], T.tr[:, 0:512:16], A.is_gt, [("tr", 0, 1024)], [("a0", 0, 64)])
         tt(T.mm[:], T.tr[:, 512:1024:16], T.tr[:, 0:512:16], A.max, [("tr", 0, 1024)], [("mm", 0, 32)])
+        spare()
         op("V", lambda: V.tensor_tensor_scan(T.w1[:], T.a0[:], T.a1[:], 0.0, A.mult, A.add),
            [("a0", 0, 64), ("a1", 0, 64)], [("w1", 0, 64)])
         tt(T.b0[:, 1:32:2], T.mm[:, 0:32:2], T.mm[:, 1:32:2], A.is_ge, [("mm", 0, 32)], [("b0", 0, 32)])
+        spare()
         tt(T.w1[:, 1:64:4], T.w1[:, 1:64:4], T.w1[:, 3:64:4], A.subtract, [("w1", 0, 64)], [("w1", 0, 64)])
+        spare()
         op("V", lambda: V.tensor_tensor_scan(T.rin[:, 0:256:8], T.b0[:], T.w1[:, 1:64:2], 0.0, A.mult, A.add),
            [("b0", 0, 32), ("w1", 0, 64)], [("rin", 0, 256)])
-        op("V", lambda: V.transpose(T.rows[:, 512:768], T.rin[:]), [("rin", 0, 256)], [("rows", 512, 768)])
-        window("S", pieces["S"][t][0])
-        table(1, T.rows[8:128:16, 512:768], [("rows", 512, 768)])
+        spare()
+        op("V", lambda: V.transpose(T.rows[:, 256:512], T.rin[:]), [("rin", 0, 256)], [("rows", 256, 512)])
+        if late:
+            window("S", PIECES[t][0])
+        table(0, T.rows[8:128:16, 256:512], [("rows", 256, 512)])
 
         steps, power = [], 1
         for i, (tb, make) in enumerate(main):
@@ -445,69 +466,79 @@ def rank_program(g, core, T, topo):
             op("V", lambda: V.transpose(T.trs[:, d:d + 128], T.rows[:, c:c + 128]), [("rows", c, c + 128)], [("trs", d, d + 128)])
 
         for i in range(len(steps) + 1):
-            if i:
-                turn(i - 1, 0)
-                turn(i - 1, 1)
-            cast(i, 0)
-            cast(i, 1)
+            us = (away, 1 - away) if i >= len(steps) - 1 else (0, 1)
+            for u in us if i else ():
+                turn(i - 1, u)
+            for u in us:
+                cast(i, u)
             if i == len(steps):
                 break
-            if i == 0:
+            if i:
+                spare()
+            else:
                 if t == 0:
                     spread_tiles(3)
-                window("S", pieces["S"][t][1])
-                window("V", pieces["V"][t][1])
-            gather(i, 0, "S")
-            gather(i, 1, "V")
+                    spare(5)
+                    unit_tiles()
+                    for z in range(2):
+                        for c in (64, 320):
+                            later.append(lambda z=z, c=c: quant("zq%d" % z, "zs%d" % z, c, 128, "x0", 0))
+                if late:
+                    window("S", PIECES[t][1])
+                    window("V", BEFORE[t])
+                else:
+                    window("S", SHARE[t][a], 512)
+            gather(i, us[0], "S" if late else "V")
+            gather(i, us[1], "V")
             row = steps[i][3]
             if steps[i][4]:
-                table(row - 1, T.rows[0:128:16, 256 * row:256 * row + 256], [("rows", 256 * row, 256 * row + 256)])
-            window("S", pieces["S"][t][i + 2])
-            window("V", pieces["V"][t][i + 2])
-        while made[0] < 16 or todo["S"] or todo["V"]:
-            window("S", 2)
-            window("V", 2)
+                table(row - 1, T.rows[0:128:16, 256 * row:256 * row + 256], [("rows", 256 * row, 256 * row + 256)], "YS" if late else "Y")
+            if late:
+                window("S", PIECES[t][i + 2])
+        window("V", 16, 512)
 
-        for b in range(4):
-            copy("VS"[b % 2], T[gt][:, b:1024:4], T.win[:, NS * b:NS * b + NS].indirect(T.offf[:]),
-                 [("win", NS * b, NS * b + NS), ("offf", 0, 16)], [(gt, b, b + 1)])
-        quant(gq, gs, 0, 256, gt, 0)
+        def fetch(u, b):
+            lo = 512 * u + b
+            copy("VS"[b % 2], T[gt][:, lo:512 * u + 512:4], T.win[:, NS * b:NS * b + NS].indirect(T.offf[:, 8 * u:8 * u + 8]),
+                 [("win", NS * b, NS * b + NS), ("offf", 8 * u, 8 * u + 8)], [(gt, lo, lo + 1)])
+
         aX = lambda s: "aX%d%d" % (t, s % 4)
-        send(aX, served, lambda d: codes(gq, 64 * (d % 4), 64 * (d % 4) + 64), lambda d: codes(zq, LAND[a], LAND[a] + 64), [(gq, 0, 256)])
-        send(aX, served, lambda d: T[gs][:, 64 * (d % 4):64 * (d % 4) + 64], lambda d: T[zs][:, LAND[a]:LAND[a] + 64], [(gs, 0, 256)])
+        for b in range(4):
+            fetch(away, b)
+        for b in (0, 1, 3):
+            fetch(1 - away, b)
+        for u in (away, 1 - away):
+            if u != away:
+                fetch(u, 2)
+            quant(gq, gs, 128 * u, 128, gt, 512 * u)
+            if u != away:
+                send(aX, served, lambda d: T[gs][:, 64 * (d % 4):64 * (d % 4) + 64], lambda d: T[zs][:, LAND[a]:LAND[a] + 64], [(gs, 0, 256)])
+            send(aX, lambda s: [d for d in served(s) if beside(s, d) == (u != away)], lambda d: codes(gq, 64 * (d % 4), 64 * (d % 4) + 64),
+                 lambda d: codes(zq, LAND[a], LAND[a] + 64), [(gq, 128 * u, 128 * u + 128)], 8)
         for c in range(4):
             if c != a:
                 arrive(aX(c), [(zq, LAND[c], LAND[c] + 64), (zs, LAND[c], LAND[c] + 64)])
 
         if t == 0:
-            unit_tiles()
-            for z in range(2):
-                for c in (64, 320):
-                    quant("zq%d" % z, "zs%d" % z, c, 128, "x0", 0)
+            spare(len(later))
         else:
             copy("V", T.prow[:], T.tab[:, NS * NAT:NS * NAT + NS].indirect(T.offf[:]),
                  [("tab", NS * NAT, NS * NAT + NS), ("offf", 0, 16)], [("prow", 0, 256)])
             dmas("dpl", [("Y", T.dpo[d % 4], T.prow[0:128:16, 64 * (d % 4):64 * (d % 4) + 64]) for d in served(r)],
                  [("prow", 0, 256)], [("dpo", 0, 4)])
-            send(lambda s: "aP", served, lambda d: T.dpo[d % 4], lambda d: T.dpi[a], [("dpo", 0, 4)], 1)
-            arrive("aP", [("dpi", 0, 4)])
+            send(lambda s: "aP%d" % (s % 4), served, lambda d: T.dpo[d % 4], lambda d: T.dpi[a], [("dpo", 0, 4)], 1)
             outs = [("Y", T.pl[2 * a:2 * a + 2, 64 * ((q - a) % 4):64 * ((q - a) % 4) + 64],
                      T.prow[32 * q:32 * q + 32:16, 64 * a:64 * a + 64]) for q in range(4)]
             dmas("own", outs, [("prow", 0, 256)], [])
-            outs = [("Y", T.pl[2 * c:2 * c + 2, 64 * ((q - c) % 4):64 * ((q - c) % 4) + 64], T.dpi[c, 32 * q:32 * q + 32, :])
-                    for c in range(4) if c != a for q in range(4)]
-            dmas("stg", outs, [("dpi", 0, 4)], [])
+            for c in range(4):
+                if c != a:
+                    arrive("aP%d" % c, [("dpi", c, c + 1)])
+                    outs = [("Y", T.pl[2 * c:2 * c + 2, 64 * ((q - c) % 4):64 * ((q - c) % 4) + 64], T.dpi[c, 32 * q:32 * q + 32, :])
+                            for q in range(4)]
+                    dmas("pl%d" % c, outs, [("dpi", c, c + 1)], [])
             quant("vq", "vs", 0, 128, "vt", 0)
 
-        def place(c, off, blks):
-            for blk in blks:
-                for b in range(4):
-                    q, lo, k = (blk + c) % 4, 256 * blk + b, 4 * (c % 2) + b
-                    copy("VS"[b % 2], T[ht][32 * c:32 * c + 32, lo:256 * blk + 256:4],
-                         T.ps[32 * q:32 * q + 32, 512 * k + off:512 * k + off + 64], [bank(k)], [(ht, lo + 4 * c, lo + 4 * c + 1)])
-
-        order = [a] + [c for c in range(4) if c != a]
-        for c in order:
+        for c in [a] + [c for c in range(4) if c != a]:
             if c == a:
                 m0 = min(64 * a, 128)
                 src, off = (gq, gs, m0), 64 * a - m0
@@ -515,19 +546,19 @@ def rank_program(g, core, T, topo):
                 src, off = (zq, zs, 128 * c), LAND[c] - 128 * c
             for b in range(4):
                 mx(4 * (c % 2) + b, "rq", "rs", 128 * b, src[0], src[1], src[2], 128)
-            place(c, off, (0, 1))
-            if c == order[-1]:
-                quant(hq, hs, 0, 128, ht, 0)
-            place(c, off, (2, 3))
+            for blk in range(4):
+                for b in range(4):
+                    q, lo, k = (blk + c) % 4, 256 * blk + b, 4 * (c % 2) + b
+                    copy("VS"[b % 2], T[ht][32 * c:32 * c + 32, lo:256 * blk + 256:4],
+                         T.ps[32 * q:32 * q + 32, 512 * k + off:512 * k + off + 64], [bank(k)], [(ht, lo + 4 * c, lo + 4 * c + 1)])
 
         Xn = "x%d" % (t + 1)
         side = ("vq", "vs") if t else ("uq", "us")
-
-        def layer(u):
+        for u in range(2):
+            quant(hq, hs, 128 * u, 128, ht, 512 * u)
             for b in range(4):
                 mx(4 * u + b, "wq", "wp", 128 * b, hq, hs, 128 * u, 128)
-
-        def relu(u):
+        for u in range(2):
             for b in range(4):
                 lo, k = 512 * u + b, 512 * (4 * u + b)
                 o, i = T[Xn][:, lo:512 * u + 512:4], T.ps[:, k:k + 128]
@@ -535,24 +566,19 @@ def rank_program(g, core, T, topo):
                     op("S", lambda: S.activation(o, i, ACT.Relu, scale=0.03125), [bank(4 * u + b)], [(Xn, lo, lo + 1)])
                 else:
                     ts(o, i, 0.0, A.max, [bank(4 * u + b)], [(Xn, lo, lo + 1)], 0.03125, A.mult)
-
-        layer(0)
-        quant(hq, hs, 128, 128, ht, 512)
-        layer(1)
-        relu(0)
         product_half(t + 1, 0, *side)
-        relu(1)
         product_half(t + 1, 1, *side)
         if t == 0:
             score_row(0, "S")
             score_row(1, "V")
 
+    dmas("ldw", [("S", T.oc[:, 0:512], codes("xq2", 0, 128))], [("xq2", 0, 128)], [])
     copy("S", T.yt[:, 0:128], T.ps[:, 0:128], [bank(0)], [("yt", 0, 128)])
-    dmas("outs", [("Y", T.oc[:], codes("xq2", 0, 256))]
-         + [("S", T.osc[4 * k:4 * k + 4, :], T.xs2[32 * k:32 * k + 4, :]) for k in range(4)],
-         [("xq2", 0, 256), ("xs2", 0, 256)], [])
+    dmas("ldv", [("Y", T.oc[:, 512:1024], codes("xq2", 128, 256))], [("xq2", 128, 256)], [])
+    dmas("ldx", [("S", T.y[:, 0:128], T.yt[:, 0:128])], [("yt", 0, 128)], [])
+    dmas("outs", [("YS"[k % 2], T.osc[4 * k:4 * k + 4, :], T.xs2[32 * k:32 * k + 4, :]) for k in range(4)], [("xs2", 0, 256)], [])
     copy("V", T.yt[:, 128:256], T.ps[:, 2048:2048 + 128], [bank(4)], [("yt", 128, 256)])
-    dmas("ldu", [("Y", T.y[:], T.yt[:])], [("yt", 0, 256)], [])
+    dmas("ldu", [("Y", T.y[:, 128:256], T.yt[:, 128:256])], [("yt", 128, 256)], [])
     for s in SEMAPHORES:
         if count[s]:
             wait("G", (s, count[s]))

from concourse.bass import DstId, RemoteDMATransfer
from concourse.mybir import dt, AluOpType, ActivationFunctionType

F32, BF, I32, U16, U8, X4 = "float32", "bfloat16", "int32", "uint16", "uint8", "float8_e4m3fn_x4"
NS = 2048
NAT = 4

SCRATCH = {
    "ps": ("psum", [128, 4096], F32),
    "tab": ("sbuf", [128, 5 * NS], F32),
    "win": ("sbuf", [128, 4 * NS], BF),
    "ut": ("sbuf", [128, 512], BF), "vt": ("sbuf", [128, 512], BF),
    "uq": ("sbuf", [128, 128], X4), "us": ("sbuf", [128, 128], U8),
    "vq": ("sbuf", [128, 128], X4), "vs": ("sbuf", [128, 128], U8),
    "wq": ("sbuf", [128, 512], X4), "wp": ("sbuf", [128, 512], U8),
    "cb": ("sbuf", [128, 520], BF), "cb2": ("sbuf", [128, 520], BF),
    "io1": ("sbuf", [128, 128], F32), "io2": ("sbuf", [128, 128], F32),
    "rq": ("sbuf", [128, 512], X4), "rs": ("sbuf", [128, 512], U8),
    "bq": ("sbuf", [128, 2048], X4), "bs": ("sbuf", [128, 2048], U8),
    "sb": ("sbuf", [128, 16, 16], I32), "sr": ("sbuf", [128, 8, 8], F32), "so": ("sbuf", [128, 8, 8], F32),
    "offs": ("sbuf", [128, 64], U16),
    "a0": ("sbuf", [128, 64], F32), "a1": ("sbuf", [128, 64], F32), "b0": ("sbuf", [128, 32], F32),
    "mm": ("sbuf", [128, 32], F32), "w1": ("sbuf", [128, 64], F32),
    "sg": ("sbuf", [128, 1024], F32), "tr": ("sbuf", [128, 1024], F32),
    "rin": ("sbuf", [128, 256], F32), "rows": ("sbuf", [128, 8 * 256], F32), "trs": ("sbuf", [128, 512], F32),
    "off": ("sbuf", [128, 64], U16), "offf": ("sbuf", [128, 16], U16),
    "pi": ("sbuf", [128, 16], I32), "tau": ("sbuf", [128, 8], F32),
    "srow": ("sbuf", [128, 256], F32), "prow": ("sbuf", [128, 256], F32), "yt": ("sbuf", [128, 256], F32),
    "dpo": ("dram", [4, 128, 4], F32), "dpi": ("dram", [4, 128, 4], F32), "dsc": ("dram", [8, 128, 8], I32),
}
for _t in range(3):
    SCRATCH["x%d" % _t] = ("sbuf", [128, 1024], BF)
    SCRATCH["xq%d" % _t] = ("sbuf", [128, 256], X4)
    SCRATCH["xs%d" % _t] = ("sbuf", [128, 256], U8)
for _t in range(2):
    SCRATCH["ds%d" % _t] = ("dram", [8 + 8 * _t, 128, 2], F32)
    SCRATCH["tl%d" % _t] = ("sbuf", [128, 1024], BF)
    SCRATCH["tq%d" % _t] = ("sbuf", [128, 256], X4)
    SCRATCH["ts%d" % _t] = ("sbuf", [128, 256], U8)
    SCRATCH["fq%d" % _t] = ("sbuf", [128, 128], X4)
    SCRATCH["fs%d" % _t] = ("sbuf", [128, 128], U8)
    SCRATCH["lq%d" % _t] = ("sbuf", [128, 512], X4)
    SCRATCH["ls%d" % _t] = ("sbuf", [128, 512], U8)
    SCRATCH["gt%d" % _t] = ("sbuf", [128, 1024], BF)
    SCRATCH["gq%d" % _t] = ("sbuf", [128, 256], X4)
    SCRATCH["gs%d" % _t] = ("sbuf", [128, 256], U8)
    SCRATCH["zq%d" % _t] = ("sbuf", [128, 512], X4)
    SCRATCH["zs%d" % _t] = ("sbuf", [128, 512], U8)
    SCRATCH["ht%d" % _t] = ("sbuf", [128, 1024], BF)
    SCRATCH["hq%d" % _t] = ("sbuf", [128, 256], X4)
    SCRATCH["hs%d" % _t] = ("sbuf", [128, 256], U8)

SEMAPHORES = (["cV", "cS", "cP", "cG", "sent", "ldx", "ldu", "lda", "ldb", "ldw", "ldv", "stg", "own", "dpl", "outs", "aC"]
              + ["tb%d" % k for k in range(4)] + ["aP%d" % k for k in range(4)] + ["pl%d" % k for k in range(4)]
              + ["aS0", "aS1", "aT0", "aT1", "hq0", "hq1", "hs0", "hs1"]
              + ["aX%d%d" % (t, c) for t in range(2) for c in range(4)])

PLAN = {0: ([], [(0, 1)], {1: 0, 0: 1}),
        1: ([(1, 0), (1, 1)], [(1, 1), (1, 3), (1, 3)], {1: 0, 3: 1}),
        2: ([(1, 0), (1, 1), (1, 0), (1, 1), (3, 0), (3, 1)], [(1, 5), (1, 5), (3, 11)], {1: 0, 3: 1, 5: 2, 11: 3}),
        3: ([(1, 0), (1, 1), (1, 0), (3, 1), (3, 0), (7, 1), (3, 0), (17, 1)], [(3, 17), (7, 37), (17, 37)],
            {1: 0, 3: 1, 7: 0, 17: 2, 37: 3})}
PIECES = [[6, 4, 3, 0, 3, 0, 3, 0, 3, 0, 3, 3, 0], [6, 4, 3, 0, 3, 0, 3, 0, 3, 0, 2, 2, 0]]
BEFORE = [4, 6]
SHARE = [(8, 12, 16), (8, 12, 15)]
LAND = [0, 192, 256, 448]


def masks(topo, src, dsts, cap=16):
    far = [d for d in dsts if topo.chip(d) != topo.chip(src)]
    near = [d for d in dsts if topo.chip(d) == topo.chip(src)]
    out, used = {}, []
    for group in (far, near):
        if not group:
            continue
        eng = [e for e in topo.engines(src, group[0]) if e not in used]
        if group is near:
            eng.reverse()
        if group is far:
            used = list(eng)
        n = [1] * len(group)
        grown = True
        while grown:
            grown = False
            for i in range(len(group)):
                if n[i] == min(n) and sum(n) + n[i] <= len(eng) and 2 * n[i] <= cap:
                    n[i] *= 2
                    grown = True
        k = 0
        for d, c in zip(group, n):
            out[d] = eng[k:k + c]
            k += c
    return out


def helpers(topo, cores, c):
    def idle(x):
        return [y for y in topo.cores_of(x) if y not in cores and topo.die(y) == topo.die(c)]
    mate = [d for d in cores if topo.mates(topo.chip(d), topo.chip(c))][0]
    here = [d for d in cores if d != c and (topo.chip(d) == topo.chip(c) or topo.same_plane(topo.chip(d), topo.chip(c)))]
    rest = [d for d in cores if d != c and d not in here]
    return {x: [d for d in to if cores.index(d) % 4 != 3] for x, to in ((idle(c)[0], here), (idle(mate)[1], rest))}


def fused(g, T, topo, src, dsts, sem, src_of, dst_of, cap=16):
    m = masks(topo, src, dsts, cap)
    tr = []
    for d in dsts:
        rid, pid, _ = topo.addr(d)
        to = dst_of(d) if isinstance(dst_of(d), list) else [dst_of(d)]
        tr.append(RemoteDMATransfer(dst_ids=[DstId(rid=rid, pnc=pid)] * len(to), dma_engine_mask=sum(1 << e for e in m[d]),
                                    remote_sem=T.sem[sem], srcs=[src_of(d)], dsts=to))
    g.remote_dma_fused(tr, local_sem=T.sem.sent)
    return sum(len(m[d]) for d in dsts)


def hand_on(g, core, T, topo):
    cores = list(T.cores)
    for s, c in enumerate(cores):
        hp = helpers(topo, cores, c)
        if core not in hp:
            continue
        n, sent = len(masks(topo, c, list(hp))[core]), 0
        lo = lambda d: 64 * (cores.index(d) % 2)
        for t in range(2):
            g.wait_ge(T.sem["hq%d" % t], n)
            sent += fused(g, T, topo, core, hp[core], "aT%d" % t, lambda d: T["fq%d" % t][:, lo(d):lo(d) + 64].bitcast(dt.uint8),
                          lambda d: T["lq%d" % t][:, 64 * s:64 * s + 64].bitcast(dt.uint8))
            g.wait_ge(T.sem["hs%d" % t], n)
            sent += fused(g, T, topo, core, hp[core], "aT%d" % t, lambda d: T["fs%d" % t][:, lo(d):lo(d) + 64],
                          lambda d: T["ls%d" % t][:, 64 * s:64 * s + 64])
        g.wait_ge(T.sem.sent, sent)


def rank_program(g, core, T, topo):
    r = T.rank_of(core)
    if r is None:
        hand_on(g, core, T, topo)
        return
    cores = list(T.cores)
    N = len(cores)
    a, h = r % 4, r // 4
    Q = {"V": g.vector, "S": g.scalar, "P": g.tensor, "Y": g.sync, "G": g}
    V, S, P = g.vector, g.scalar, g.tensor
    A, ACT = AluOpType, ActivationFunctionType
    count = {s: 0 for s in SEMAPHORES}
    waited = {q: {} for q in Q}
    acc = {}

    def wait(q, tok):
        if waited[q].get(tok[0], 0) < tok[1]:
            Q[q].wait_ge(T.sem[tok[0]], tok[1])
            waited[q][tok[0]] = tok[1]

    def need(q, reads, writes):
        want = {}
        for (b, lo, hi), w in [(x, False) for x in reads] + [(x, True) for x in writes]:
            for l2, h2, w2, tok in acc.get(b, []):
                if l2 < hi and lo < h2 and (w or w2):
                    want[tok[0]] = max(want.get(tok[0], 0), tok[1])
        for s in want:
            wait(q, (s, want[s]))

    def note(reads, writes, tok):
        for b, lo, hi in writes:
            acc[b] = [e for e in acc.get(b, []) if not (lo <= e[0] and e[1] <= hi)] + [(lo, hi, True, tok)]
        for b, lo, hi in reads:
            acc.setdefault(b, []).append((lo, hi, False, tok))

    def op(q, call, reads, writes):
        ex = [x for x in reads if x[0] == "ps"]
        reads = [x for x in reads if x[0] != "ps"]
        other = [x for x in ex if any(l2 < x[2] and x[1] < h2 and tok[0] != "c" + q for l2, h2, w2, tok in acc.get("ps", []))]
        need(q, reads, list(writes) + other)
        s = "c" + q
        count[s] += 1
        call().then_inc(T.sem[s], 1)
        note(reads, list(writes) + ex, (s, count[s]))

    def dmas(sem, items, reads, writes):
        for q in sorted({it[0] for it in items}):
            need(q, reads, writes)
            if count[sem]:
                wait(q, (sem, count[sem]))
        for q, o, i in items:
            Q[q].dma_start(o, i).then_inc(T.sem[sem], 16)
            count[sem] += 16
        note(reads, writes, (sem, count[sem]))

    def send(sem, peers, src_of, dst_of, reads, cap=16):
        need("G", reads, [])
        count["sent"] += fused(g, T, topo, core, [cores[d] for d in peers(r)], sem(r),
                               lambda c: src_of(cores.index(c)), lambda c: dst_of(cores.index(c)), cap)
        for s in range(N):
            if r in peers(s):
                count[sem(s)] += len(masks(topo, cores[s], [cores[d] for d in peers(s)], cap)[core])

    def arrive(sem, writes):
        for b, lo, hi in writes:
            acc.setdefault(b, []).append((lo, hi, True, (sem, count[sem])))

    def everyone(s):
        return [(s + k) % N for k in range(1, N)]

    def served(s):
        return [4 * (s // 4) + (s + k) % 4 for k in range(1, 4)]

    def last(s):
        return [d for d in everyone(s) if d % 4 == 3]

    def beside(s, d):
        return topo.chip(cores[s]) == topo.chip(cores[d])

    def bank(k):
        return ("ps", 512 * k, 512 * k + 512)

    def quant(qn, sn, c0, n, src, s0):
        op("V", lambda: V.quantize_mx(T[qn][:, c0:c0 + n], T[sn][:, c0:c0 + n], T[src][:, s0:s0 + 4 * n]),
           [(src, s0, s0 + 4 * n)], [(qn, c0, c0 + n), (sn, c0, c0 + n)])

    def mx(k, lq, ls, l0, mq, ms, m0, n):
        op("P", lambda: P.matmul_mx(T.ps[:, 512 * k:512 * k + n], T[lq][:, l0:l0 + 128], T[ls][:, l0:l0 + 128],
                                    T[mq][:, m0:m0 + n], T[ms][:, m0:m0 + n], True, True),
           [(lq, l0, l0 + 128), (ls, l0, l0 + 128), (mq, m0, m0 + n), (ms, m0, m0 + n)], [bank(k)])

    def copy(q, o, i, reads, writes):
        if q == "V":
            op("V", lambda: V.tensor_copy(o, i), reads, writes)
        else:
            op("S", lambda: S.activation(o, i, ACT.Copy), reads, writes)

    def ts(o, i, s1, o1, reads, writes, s2=None, o2=None):
        if o2 is None:
            op("V", lambda: V.tensor_scalar(o, i, s1, None, o1), reads, writes)
        else:
            op("V", lambda: V.tensor_scalar(o, i, s1, s2, o1, o2), reads, writes)

    def tt(o, i0, i1, o1, reads, writes):
        op("V", lambda: V.tensor_tensor(o, i0, i1, o1), reads, writes)

    def fill(name, lo, hi, c):
        op("V", lambda: V.memset(T[name][:, lo:hi], c), [], [(name, lo, hi)])

    def iota(name, lo, hi, pattern, base, cm, flt=True):
        if flt:
            op("G", lambda: g.iota(T[name][:, lo:hi], pattern, base, cm, allow_small_or_imprecise_dtypes=True), [], [(name, lo, hi)])
        else:
            op("G", lambda: g.iota(T[name][:, lo:hi], pattern, base, cm), [], [(name, lo, hi)])

    def codes(name, lo, hi):
        return T[name][:, lo:hi].bitcast(dt.uint8)

    def whole(name):
        return (name, 0, 1 << 20)

    main, branch, slot = PLAN[a]
    nmain = len(main)
    late = a == 3
    hp = helpers(topo, cores, core)
    away = [d % 4 // 2 for d in served(r) if not beside(r, d)][0]

    dmas("lda", [("YS"[y], T.dsc[r, 64 * y:64 * y + 64, :], T.sc[:, 32 * y:32 * y + 32]) for y in range(2)], [], [("dsc", r, r + 1)])
    dmas("ldu", [("S", T.ut[:], T.u[:])], [], [("ut", 0, 512)])
    dmas("ldx", [("Y", T.x0[:], T.x[:])], [], [("x0", 0, 1024)])
    iota("io2", 0, 128, [[0, 4], [-1, 32]], 0, 1)
    iota("tab", 0, 64 * (4 - a), [[512, 4 - a], [1, 64]], 512 * a, 0)
    if a:
        iota("tab", 64 * (4 - a), 256, [[512, a], [1, 64]], 0, 0)
    iota("pi", 0, 16, [[0, 16]], 0, 1, False)
    send(lambda s: "aC", everyone, lambda d: T.dsc[r], lambda d: T.dsc[r], [("dsc", r, r + 1)], 1)
    arrive("aC", [("dsc", 0, N)])
    for n in (256, 512, 1024):
        op("S", lambda: S.activation(T.tab[:, n:2 * n], T.tab[:, 0:n], ACT.Identity, bias=float(n // 4)), [("tab", 0, n)], [("tab", n, 2 * n)])

    later = []

    def spare(n=1):
        for k in range(min(n, len(later))):
            later.pop(0)()

    def spread_tiles(q):
        later.append(lambda: ts(T.cb2[:, 3:515:4], T.io2[:], float(32 * q), A.is_equal, [("io2", 0, 128)], [("cb2", 0, 520)]))
        for b in range(4):
            later.append(lambda b=b: quant("bq", "bs", 128 * (4 * q + b), 128, "cb2", 3 - b))

    def unit_tiles():
        later.append(lambda: fill("cb", 0, 520, 0.0))
        later.append(lambda: ts(T.cb[:, 3:515:4], T.io1[:], 0.0, A.is_equal, [("io1", 0, 128)], [("cb", 0, 520)]))
        for b in range(4):
            later.append(lambda b=b: quant("rq", "rs", 128 * b, 128, "cb", 3 - b))

    def table(k, src_of, reads, queues="YS"):
        dmas("tb%d" % k, [(queues[G % len(queues)], T.tab[16 * G:16 * G + 1, NS * k:NS * k + NS], src_of) for G in range(8)],
             reads, [("tab", NS * k, NS * k + NS)])

    def product_half(t, u, q, s):
        quant("xq%d" % t, "xs%d" % t, 128 * u, 128, "x%d" % t, 512 * u)
        mx(4 * u, q, s, 0, "xq%d" % t, "xs%d" % t, 128 * u, 128)

    def score_row(u, q):
        copy(q, T.srow[0:1, 128 * u:128 * u + 128], T.ps[0:1, 2048 * u:2048 * u + 128], [bank(4 * u)], [("srow", 128 * u, 128 * u + 128)])

    fill("cb2", 0, 520, 0.0)
    fill("a0", 0, 64, 0.0)
    fill("b0", 0, 32, 0.0)
    fill("rin", 0, 256, 0.0)
    spread_tiles(0)
    spare(5)
    quant("uq", "us", 0, 128, "ut", 0)
    product_half(0, 0, "uq", "us")
    product_half(0, 1, "uq", "us")
    score_row(0, "V")
    score_row(1, "V")

    for t in range(2):
        X, ds = "x%d" % t, "ds%d" % t
        tl, tq, tsc, lq, ls = "tl%d" % t, "tq%d" % t, "ts%d" % t, "lq%d" % t, "ls%d" % t
        gt, gq, gs, zq, zs = "gt%d" % t, "gq%d" % t, "gs%d" % t, "zq%d" % t, "zs%d" % t
        ht, hq, hs = "ht%d" % t, "hq%d" % t, "hs%d" % t

        dmas("stg", [("Y", T[ds][r], T.srow[0:1, :])], [("srow", 0, 256)], [(ds, r, r + 1)])
        if t:
            dmas("dpl", [("Y", T[ds][N + r], T.srow[0:1, :])], [("srow", 0, 256)], [(ds, N + r, N + r + 1)])
        send(lambda s: "aS%d" % t, everyone, lambda d: T[ds][r], lambda d: [T[ds][N * k + r] for k in range(1 + t)], [(ds, r, r + 1)], 1)
        count["aS%d" % t] *= 1 + t
        arrive("aS%d" % t, [(ds, 0, 2 * N)])

        n = 0
        for c in (3, 2, 1, 0):
            for q in range(4):
                blk = (q - c) % 4
                eng = "S" if n % 3 == 2 else "V"
                n += 1
                lo = 256 * c + q
                copy(eng, T[tl][32 * q:32 * q + 32, 256 * c:256 * c + 256], T[X][32 * c:32 * c + 32, 256 * blk:256 * blk + 256],
                     [(X, 0, 1024)], [(tl, lo, lo + 1)])
            if c % 2 == 0:
                quant(tq, tsc, 64 * c, 128, tl, 256 * c)
            if c == 2:
                send(lambda s: "aT%d" % t, last, lambda d: codes(tq, 192, 256), lambda d: codes(lq, 64 * r, 64 * r + 64), [(tq, 128, 256)])
                send(lambda s: "aT%d" % t, last, lambda d: T[tsc][:, 192:256], lambda d: T[ls][:, 64 * r:64 * r + 64], [(tsc, 128, 256)])
        need("G", [(tq, 0, 256), (tsc, 0, 256)], [])
        pair = lambda c: 128 * (cores.index(hp[c][0]) % 4 // 2)
        count["sent"] += fused(g, T, topo, core, list(hp), "hq%d" % t, lambda c: codes(tq, pair(c), pair(c) + 128),
                               lambda c: codes("fq%d" % t, 0, 128))
        count["sent"] += fused(g, T, topo, core, list(hp), "hs%d" % t, lambda c: T[tsc][:, pair(c):pair(c) + 128],
                               lambda c: T["fs%d" % t][:])
        for c in cores:
            for hc, to in helpers(topo, cores, c).items():
                if core in to:
                    count["aT%d" % t] += 2 * len(masks(topo, hc, to)[core])

        if t == 0:
            dmas("ldb", [("YS"[s % 2], T.sb[0:32, 4 * (s % 4) + 2 * (s // 4):4 * (s % 4) + 2 * (s // 4) + 2, :], T.dsc[s])
                         for s in range(N)], [("dsc", 0, N)], [whole("sb")])
            table(0, T[ds][:], [(ds, 0, N)])
        else:
            dmas("tb0", [("YS"[q % 2], T.tab[32 * q:32 * q + 32:16, 0:NS], T[ds][:]) for q in range(4)], [(ds, 0, 2 * N)], [("tab", 0, NS)])
        dmas("own", [("Y", codes(lq, 64 * r, 64 * r + 64), codes(tq, 64 * a, 64 * a + 64)),
                     ("Y", T[ls][:, 64 * r:64 * r + 64], T[tsc][:, 64 * a:64 * a + 64])],
             [(tq, 0, 256), (tsc, 0, 256)], [(lq, 64 * r, 64 * r + 64), (ls, 64 * r, 64 * r + 64)])
        arrive("aT%d" % t, [(lq, 0, 512), (ls, 0, 512)])

        if t == 0:
            dmas("ldw", [("Y", codes("wq", 0, 512), T.wc[:]), ("Y", T.wp[:], T.ws[:])], [], [("wq", 0, 512), ("wp", 0, 512)])
            for k in sorted(set(slot.values()) - {0}):
                iota("tab", NS * k, NS * k + NS, [[1, NS]], 0, 0)
                if k == 1:
                    iota("io1", 0, 128, [[-1, 128]], 0, 1)
            ts(T.pi[:, 8:16], T.pi[:, 0:8], 4, A.logical_shift_right, [("pi", 0, 8)], [("pi", 8, 16)], 1, A.bitwise_and)
            spread_tiles(1)
            spread_tiles(2)
            spare(6)
            if len(branch) > 1:
                s0, s1 = slot[branch[1][0]], slot[branch[1][1]]
                ts(T.tau[:, 0:1], T.pi[:, 8:9], float(NS * (s1 - s0)), A.mult, [("pi", 8, 16)], [("tau", 0, 1)],
                   float(NS * (s0 - min(s0, s1))), A.add)
            for q in range(4):
                blk = (q - a) % 4
                copy("V", T.sr[32 * q:32 * q + 32, :, :], T.sb[0:32, :, 4 * blk:4 * blk + 4], [whole("sb")], [("sr", q, q + 1)])
            for k1 in range(2):
                for cb in range(2):
                    c = 4 * k1 + 2 * cb
                    copy("V", T.so[:, 4 * k1:4 * k1 + 4, 4 * cb:4 * cb + 4], T.sr[:, :, c:c + 2], [whole("sr")], [("so", c, c + 1)])
            copy("V", T.offs[:], T.so[:], [whole("so")], [("offs", 0, 64)])
        else:
            dmas("ldv", [("Y", T.vt[:], T.v[:])], [], [("vt", 0, 512)])
            for q in range(4):
                lo = NS * NAT + 512 * q
                iota("tab", lo, lo + 512, [[256, 8], [1, 64]], 64 * ((q - a) % 4), 0)

        made, todo = [0], {"S": [], "V": []}

        def window(q, m, w=256):
            for j in range(m):
                if not todo[q]:
                    if made[0] == 16:
                        return
                    n = made[0]
                    made[0] += 1
                    mx(n % 8, "bq", "bs", 128 * n, lq, ls, 0, 512)
                    todo[q] = [(n, c) for c in range(0, 512, w)]
                n, c = todo[q].pop(0)
                lo, k = NS * (n % 4) + 512 * (n // 4) + c, 512 * (n % 8) + c
                copy(q, T.win[:, lo:lo + w], T.ps[:, k:k + w], [bank(n % 8)], [("win", lo, lo + w)])

        for q, lo, hi in (("V", 0, 16), ("S", 16, 32), ("S", 32, 48), ("V", 56, 64), ("S", 48, 56)):
            copy(q, T.sg[:, 16 * lo:16 * hi], T.tab[:, 0:NS].indirect(T.offs[:, lo:hi]),
                 [("tab", 0, NS), ("offs", 0, 64)], [("sg", 16 * lo, 16 * hi)])
        for k in range(4):
            op("V", lambda: V.transpose(T.tr[:, 256 * k:256 * k + 256], T.sg[:, 256 * k:256 * k + 256]),
               [("sg", 256 * k, 256 * k + 256)], [("tr", 256 * k, 256 * k + 256)])
        if t == 0:
            tt(T.a1[:, 0:64:2], T.tr[:, 513:1024:16], T.tr[:, 1:512:16], A.subtract, [("tr", 0, 1024)], [("a1", 0, 1)])
            copy("V", T.a1[:, 1:64:2], T.tr[:, 1:512:16], [("tr", 0, 1024)], [("a1", 1, 2)])
        tt(T.a0[:, 1:64:2], T.tr[:, 512:1024:16], T.tr[:, 0:512:16], A.is_gt, [("tr", 0, 1024)], [("a0", 0, 64)])
        tt(T.mm[:], T.tr[:, 512:1024:16], T.tr[:, 0:512:16], A.max, [("tr", 0, 1024)], [("mm", 0, 32)])
        spare()
        op("V", lambda: V.tensor_tensor_scan(T.w1[:], T.a0[:], T.a1[:], 0.0, A.mult, A.add),
           [("a0", 0, 64), ("a1", 0, 64)], [("w1", 0, 64)])
        tt(T.b0[:, 1:32:2], T.mm[:, 0:32:2], T.mm[:, 1:32:2], A.is_ge, [("mm", 0, 32)], [("b0", 0, 32)])
        spare()
        tt(T.w1[:, 1:64:4], T.w1[:, 1:64:4], T.w1[:, 3:64:4], A.subtract, [("w1", 0, 64)], [("w1", 0, 64)])
        spare()
        op("V", lambda: V.tensor_tensor_scan(T.rin[:, 0:256:8], T.b0[:], T.w1[:, 1:64:2], 0.0, A.mult, A.add),
           [("b0", 0, 32), ("w1", 0, 64)], [("rin", 0, 256)])
        spare()
        op("V", lambda: V.transpose(T.rows[:, 256:512], T.rin[:]), [("rin", 0, 256)], [("rows", 256, 512)])
        if late:
            window("S", PIECES[t][0])
        table(0, T.rows[8:128:16, 256:512], [("rows", 256, 512)])

        steps, power = [], 1
        for i, (tb, make) in enumerate(main):
            power += tb
            steps.append(("plain", slot[tb], slot[tb], 1 + slot[power] if make else 0, make))
        for k, (p0, p1) in enumerate(branch):
            steps.append((("first", "group", "column")[k], slot[p0], slot[p1], 6 + k % 2, 0))

        def cast(i, u):
            buf, base, c0 = ("trs", 256 * ((i - 1) % 2), 0) if i and (i, a) != (nmain, 1) else ("rin", 0, 8)
            lo = base + 128 * u
            rd = [(buf, lo, lo + 128)]
            if i == len(steps):
                copy("V", T.offf[:, 8 * u:8 * u + 8], T[buf][:, lo + c0:lo + 128:16], rd, [("offf", 8 * u, 8 * u + 8)])
                return
            kind, s0, s1 = steps[i][:3]
            oc, first = 16 * (i % 2) + 8 * u, min(s0, s1)
            if kind == "plain":
                copy("V", T.off[:, oc:oc + 8], T[buf][:, lo + c0:lo + 128:16], rd, [("off", oc, oc + 8)])
            elif kind == "group":
                ts(T.off[:, oc:oc + 8], T[buf][:, lo + c0:lo + 128:16], T.tau[:, 0:1], A.add, rd + [("tau", 0, 1)], [("off", oc, oc + 8)])
            else:
                for w, s in ((0, s0), (1, s1)):
                    c = lo + c0 + 16 * (h if kind == "first" else w)
                    ts(T.off[:, oc + w:oc + 8:2], T[buf][:, c:lo + 128:32], float(NS * (s - first)), A.add, rd, [("off", oc + w, oc + w + 1)])

        def gather(i, u, q):
            kind, s0, s1, row = steps[i][:4]
            oc, lo, hi, c = 16 * (i % 2) + 8 * u, NS * min(s0, s1), NS * max(s0, s1) + NS, 256 * row + 128 * u
            copy(q, T.rows[:, c:c + 128], T.tab[:, lo:hi].indirect(T.off[:, oc:oc + 8]),
                 [("tab", lo, hi), ("off", oc, oc + 8)], [("rows", c, c + 128)])

        def turn(i, u):
            c, d = 256 * steps[i][3] + 128 * u, 256 * (i % 2) + 128 * u
            op("V", lambda: V.transpose(T.trs[:, d:d + 128], T.rows[:, c:c + 128]), [("rows", c, c + 128)], [("trs", d, d + 128)])

        for i in range(len(steps) + 1):
            us = (away, 1 - away) if i >= len(steps) - 1 else (0, 1)
            for u in us if i else ():
                turn(i - 1, u)
            for u in us:
                cast(i, u)
            if i == len(steps):
                break
            if i:
                spare()
            else:
                if t == 0:
                    spread_tiles(3)
                    spare(5)
                    unit_tiles()
                    for z in range(2):
                        for c in (64, 320):
                            later.append(lambda z=z, c=c: quant("zq%d" % z, "zs%d" % z, c, 128, "x0", 0))
                if late:
                    window("S", PIECES[t][1])
                    window("V", BEFORE[t])
                else:
                    window("S", SHARE[t][a], 512)
            gather(i, us[0], "S" if late else "V")
            gather(i, us[1], "V")
            row = steps[i][3]
            if steps[i][4]:
                table(row - 1, T.rows[0:128:16, 256 * row:256 * row + 256], [("rows", 256 * row, 256 * row + 256)], "YS" if late else "Y")
            if late:
                window("S", PIECES[t][i + 2])
        window("V", 16, 512)

        def fetch(u, b):
            lo = 512 * u + b
            copy("VS"[b % 2], T[gt][:, lo:512 * u + 512:4], T.win[:, NS * b:NS * b + NS].indirect(T.offf[:, 8 * u:8 * u + 8]),
                 [("win", NS * b, NS * b + NS), ("offf", 8 * u, 8 * u + 8)], [(gt, lo, lo + 1)])

        aX = lambda s: "aX%d%d" % (t, s % 4)
        for b in range(4):
            fetch(away, b)
        for b in (0, 1, 3):
            fetch(1 - away, b)
        for u in (away, 1 - away):
            if u != away:
                fetch(u, 2)
            quant(gq, gs, 128 * u, 128, gt, 512 * u)
            if u != away:
                send(aX, served, lambda d: T[gs][:, 64 * (d % 4):64 * (d % 4) + 64], lambda d: T[zs][:, LAND[a]:LAND[a] + 64], [(gs, 0, 256)])
            send(aX, lambda s: [d for d in served(s) if beside(s, d) == (u != away)], lambda d: codes(gq, 64 * (d % 4), 64 * (d % 4) + 64),
                 lambda d: codes(zq, LAND[a], LAND[a] + 64), [(gq, 128 * u, 128 * u + 128)], 8)
        for c in range(4):
            if c != a:
                arrive(aX(c), [(zq, LAND[c], LAND[c] + 64), (zs, LAND[c], LAND[c] + 64)])

        if t == 0:
            spare(len(later))
        else:
            copy("V", T.prow[:], T.tab[:, NS * NAT:NS * NAT + NS].indirect(T.offf[:]),
                 [("tab", NS * NAT, NS * NAT + NS), ("offf", 0, 16)], [("prow", 0, 256)])
            dmas("dpl", [("Y", T.dpo[d % 4], T.prow[0:128:16, 64 * (d % 4):64 * (d % 4) + 64]) for d in served(r)],
                 [("prow", 0, 256)], [("dpo", 0, 4)])
            send(lambda s: "aP%d" % (s % 4), served, lambda d: T.dpo[d % 4], lambda d: T.dpi[a], [("dpo", 0, 4)], 1)
            outs = [("Y", T.pl[2 * a:2 * a + 2, 64 * ((q - a) % 4):64 * ((q - a) % 4) + 64],
                     T.prow[32 * q:32 * q + 32:16, 64 * a:64 * a + 64]) for q in range(4)]
            dmas("own", outs, [("prow", 0, 256)], [])
            for c in range(4):
                if c != a:
                    arrive("aP%d" % c, [("dpi", c, c + 1)])
                    outs = [("Y", T.pl[2 * c:2 * c + 2, 64 * ((q - c) % 4):64 * ((q - c) % 4) + 64], T.dpi[c, 32 * q:32 * q + 32, :])
                            for q in range(4)]
                    dmas("pl%d" % c, outs, [("dpi", c, c + 1)], [])
            quant("vq", "vs", 0, 128, "vt", 0)

        for c in [a] + [c for c in range(4) if c != a]:
            if c == a:
                m0 = min(64 * a, 128)
                src, off = (gq, gs, m0), 64 * a - m0
            else:
                src, off = (zq, zs, 128 * c), LAND[c] - 128 * c
            for b in range(4):
                mx(4 * (c % 2) + b, "rq", "rs", 128 * b, src[0], src[1], src[2], 128)
            for blk in range(4):
                for b in range(4):
                    q, lo, k = (blk + c) % 4, 256 * blk + b, 4 * (c % 2) + b
                    copy("VS"[b % 2], T[ht][32 * c:32 * c + 32, lo:256 * blk + 256:4],
                         T.ps[32 * q:32 * q + 32, 512 * k + off:512 * k + off + 64], [bank(k)], [(ht, lo + 4 * c, lo + 4 * c + 1)])

        Xn = "x%d" % (t + 1)
        side = ("vq", "vs") if t else ("uq", "us")
        for u in range(2):
            quant(hq, hs, 128 * u, 128, ht, 512 * u)
            for b in range(4):
                mx(4 * u + b, "wq", "wp", 128 * b, hq, hs, 128 * u, 128)
        for u in range(2):
            for b in range(4):
                lo, k = 512 * u + b, 512 * (4 * u + b)
                o, i = T[Xn][:, lo:512 * u + 512:4], T.ps[:, k:k + 128]
                if b % 2 == 0:
                    op("S", lambda: S.activation(o, i, ACT.Relu, scale=0.03125), [bank(4 * u + b)], [(Xn, lo, lo + 1)])
                else:
                    ts(o, i, 0.0, A.max, [bank(4 * u + b)], [(Xn, lo, lo + 1)], 0.03125, A.mult)
        product_half(t + 1, 0, *side)
        product_half(t + 1, 1, *side)
        if t == 0:
            score_row(0, "S")
            score_row(1, "V")

    dmas("ldw", [("S", T.oc[:, 0:512], codes("xq2", 0, 128))], [("xq2", 0, 128)], [])
    copy("S", T.yt[:, 0:128], T.ps[:, 0:128], [bank(0)], [("yt", 0, 128)])
    dmas("ldv", [("Y", T.oc[:, 512:1024], codes("xq2", 128, 256))], [("xq2", 128, 256)], [])
    dmas("ldx", [("S", T.y[:, 0:128], T.yt[:, 0:128])], [("yt", 0, 128)], [])
    dmas("outs", [("YS"[k % 2], T.osc[4 * k:4 * k + 4, :], T.xs2[32 * k:32 * k + 4, :]) for k in range(4)], [("xs2", 0, 256)], [])
    copy("V", T.yt[:, 128:256], T.ps[:, 2048:2048 + 128], [bank(4)], [("yt", 128, 256)])
    dmas("ldu", [("Y", T.y[:, 128:256], T.yt[:, 128:256])], [("yt", 128, 256)], [])
    for s in SEMAPHORES:
        if count[s]:
            wait("G", (s, count[s]))
